import numpy as np
import ml_dtypes


def mxq(x, axis, fmt="e4m3"):
    dtype, down = {"e4m3": (ml_dtypes.float8_e4m3fn, 7), "e5m2": (ml_dtypes.float8_e5m2, 14)}[fmt]
    v = np.moveaxis(np.asarray(x, np.float32).astype(ml_dtypes.bfloat16).astype(np.float64), axis, -1)
    blocks = v.reshape(v.shape[:-1] + (-1, 32))
    amax = np.abs(blocks).max(-1, keepdims=True)
    byte = np.maximum(np.where(amax > 0, np.frexp(amax)[1] - 1 + 127, 0) - down, 1)
    scale = np.exp2(byte - 127.0)
    codes = (blocks / scale).astype(np.float32).astype(dtype).astype(np.float64)
    return np.moveaxis((codes * scale).reshape(v.shape), -1, axis)


WIDE = False


def mx_kscale(k):
    if not WIDE:
        return np.ones(k)
    levels = np.array([10, -10, 5, -5, 0])
    if k % 512:
        return np.exp2(np.random.permutation(np.resize(levels, k // 32))).repeat(32)
    a = np.empty((k // 512, 16))
    for p in range(k // 512):
        a[p, :8] = np.random.permutation(np.resize(levels, 8))
        for g in range(8):
            far = levels[np.abs(levels - a[p, g]) >= 10]
            a[p, g + 8] = far[np.random.randint(len(far))]
    return np.exp2(a.ravel()).repeat(32)


def f64(x):
    return np.asarray(x).astype(np.float64)


E2M1 = np.array([0.0, 0.5, 1.0, 1.5, 2.0, 3.0, 4.0, 6.0, -0.0, -0.5, -1.0, -1.5, -2.0, -3.0, -4.0, -6.0])


def pack_weight(w, fmt):
    k, n = w.shape
    w = f64(np.asarray(w, np.float32).astype(ml_dtypes.bfloat16)).reshape(k // 32, 32, n)
    amax = np.abs(w).max(1)
    if fmt == "e4m3":
        byte = np.frexp(amax)[1] - 1 + 127 - 7
    else:
        mant, ex = np.frexp(amax / 6.0)
        byte = np.where(mant > 0.5, ex, ex - 1) + 127
    byte = np.clip(np.where(amax > 0, byte, 1), 1, 254)
    scaled = (w * np.exp2(127.0 - byte)[:, None, :]).reshape(k, n).astype(np.float32)
    by_word = np.ascontiguousarray(scaled.reshape(k // 512, 128, 4, n).transpose(0, 1, 3, 2))
    if fmt == "e4m3":
        words = by_word.astype(ml_dtypes.float8_e4m3fn).view(np.uint8)
    else:
        c = by_word.astype(ml_dtypes.float4_e2m1fn).view(np.uint8) & 0xF
        words = (c[..., 0::2] | (c[..., 1::2] << 4)).reshape(k // 512, 128, 2 * n)
    return np.ascontiguousarray(words), np.ascontiguousarray(byte.astype(np.uint8).reshape(k // 512, 16, n))


def unpack_weight(words, scales, fmt):
    g, _, n = scales.shape
    words = np.ascontiguousarray(words).reshape(g, 128, n, -1)
    if fmt == "e4m3":
        vals = words.view(ml_dtypes.float8_e4m3fn).astype(np.float64)
    else:
        nib = np.empty((g, 128, n, 4), np.uint8)
        nib[..., 0::2] = words & 0xF
        nib[..., 1::2] = words >> 4
        vals = E2M1[nib]
    vals = vals * np.repeat(np.exp2(scales.astype(np.float64) - 127.0), 8, axis=1)[..., None]
    return vals.transpose(0, 1, 3, 2).reshape(g * 512, n)


def planes(y):
    n, m = y.shape
    v = y.astype(np.float32).astype(ml_dtypes.bfloat16).astype(np.float64).reshape(n // 32, 32, m)
    top = np.abs(v).max(1)
    byte = np.clip(np.where(top > 0, np.frexp(top)[1] - 1 + 127 - 7, 1), 1, 254)
    codes = (v * np.exp2(127.0 - byte)[:, None, :]).reshape(n, m).astype(np.float32).astype(ml_dtypes.float8_e4m3fn).view(np.uint8)
    words = codes.reshape(n // 512, 128, 4, m).transpose(0, 1, 3, 2)
    return np.ascontiguousarray(words), np.ascontiguousarray(byte.astype(np.uint8).reshape(n // 512, 16, m))


K, M, T = 1536, 512, 1536


def setup_inputs():
    n = np.random.standard_normal
    s = mx_kscale(K)[:, None]
    x = n((K, T)) * s
    x4 = pack_weight(x, "e2m1")
    rest = x - unpack_weight(*x4, "e2m1")
    p_w4 = pack_weight(n((K, M)) / np.sqrt(K) / s, "e2m1")
    return {
        "x4_words": x4[0],
        "x4_scales": x4[1],
        "xr": (rest).astype(np.float32),
        "w4_words": p_w4[0],
        "w4_scales": p_w4[1],
        "g": (n((1536, 512))).astype(np.float32),
    }


def reference(x4_words, x4_scales, xr, w4_words, w4_scales, g):
    x4_ = unpack_weight(x4_words, x4_scales, "e2m1")
    xr_ = mxq(f64(xr), 0, "e4m3")
    w4_ = unpack_weight(w4_words, w4_scales, "e2m1")
    y = x4_.T @ w4_ + xr_.T @ w4_
    out_0 = f64(g) * y
    return (out_0,) + planes(out_0)

@@ -1,0 +1,212 @@
+from contextlib import ExitStack
+
+import concourse.mybir as mybir
+from concourse.masks import make_identity
+
+K, M, T = 1536, 512, 1536
+FLOPS = 2 * 2 * K * M * T
+
+F32 = mybir.dt.float32
+BF16 = mybir.dt.bfloat16
+I32 = mybir.dt.int32
+U32 = mybir.dt.uint32
+U8 = mybir.dt.uint8
+FP8X4 = mybir.dt.float8_e4m3fn_x4
+FP4X4 = mybir.dt.float4_e2m1fn_x4
+
+P = 128
+PACK = 4
+SPAN = P * PACK
+PASSES = K // SPAN
+CHUNKS = T // SPAN
+NT = M // P
+VCOLS = 352
+
+
+def tile_mix_xres_tm_pl_mul_kernel(
+    tc, x4_words, x4_scales, xr, w4_words, w4_scales, g, out_0, out_1, out_2
+):
+    nc = tc.nc
+    with ExitStack() as ctx:
+        keep = ctx.enter_context(tc.tile_pool(name="keep", bufs=1))
+        stage = ctx.enter_context(tc.tile_pool(name="stage", bufs=3))
+        psum = ctx.enter_context(tc.psum_pool(name="psum", bufs=1))
+        ctx.enter_context(tc.manual_schedule())
+
+        def kept(name, shape, dtype):
+            return keep.tile(shape, dtype, name=name, align_bytes=64)
+
+        w_codes = kept("w_codes", [P, PASSES, 2 * M], U8)
+        w_scale = kept("w_scale", [P, PASSES, M], U8)
+        x4_codes = kept("x4_codes", [P, PASSES, 2 * T], U8)
+        x4_scale = kept("x4_scale", [P, PASSES, T], U8)
+        ident = kept("ident", [P, P], F32)
+        pieces = [(c, a) for c in range(CHUNKS) for a in range(PASSES)]
+        xr_raw = {ca: kept("xr_raw%d%d" % ca, [P, PACK, SPAN], F32) for ca in pieces}
+        xr_codes = {ca: kept("xr_codes%d%d" % ca, [P, SPAN], U32) for ca in pieces}
+        xr_scale = {ca: kept("xr_scale%d%d" % ca, [P, SPAN], U8) for ca in pieces}
+        g_sb = [kept("g_sb%d" % c, [P, PACK, M], F32) for c in range(CHUNKS)]
+        y_t = {(c, b): kept("y_t%d%d" % (c, b), [P, PACK, P], F32) for c in range(CHUNKS) for b in range(NT)}
+        res = [kept("res%d" % c, [P, PACK, M], F32) for c in range(CHUNKS)]
+        res_bf = [kept("res_bf%d" % c, [P, M, PACK], BF16) for c in range(CHUNKS)]
+        res_codes = [kept("res_codes%d" % c, [P, M], U32) for c in range(CHUNKS)]
+        res_scale = kept("res_scale", [P, CHUNKS, M], U8)
+        banks = [psum.tile([P, SPAN], F32, name="bank%d" % i) for i in range(2 * NT)]
+
+        def sum_bank(c, b):
+            return banks[NT * (c % 2) + b]
+
+        def turn_bank(c, b):
+            return banks[(0 if c == CHUNKS - 1 else NT) + b]
+
+        nc.vector.memset(x4_scale[:].bitcast(I32), 0)
+        nc.vector.memset(w_scale[:].bitcast(I32), 0)
+        make_identity(nc, ident[:])
+
+        def load_scales(plane, rows):
+            by_r = rows.rearrange("a (q r) n -> r q a n", r=4)
+            for r in range(4):
+                nc.sync.dma_start(out=plane[:].bitcast(I32)[r:P:32], in_=by_r[r].bitcast(I32))
+
+        nc.sync.dma_start(out=w_codes[:].bitcast(I32), in_=w4_words.rearrange("a p c -> p a c").bitcast(I32))
+        load_scales(x4_scale, x4_scales)
+        nc.sync.dma_start(out=x4_codes[:].bitcast(I32), in_=x4_words.rearrange("a p c -> p a c").bitcast(I32))
+        load_scales(w_scale, w4_scales)
+        for c, a in pieces:
+            rows = xr[a * SPAN : (a + 1) * SPAN, c * SPAN : (c + 1) * SPAN]
+            nc.sync.dma_start(out=xr_raw[c, a][:], in_=rows.rearrange("(p j) t -> p j t", j=PACK))
+        for c in range(CHUNKS):
+            rows = g[c * SPAN : (c + 1) * SPAN, :]
+            nc.sync.dma_start(out=g_sb[c][:], in_=rows.rearrange("(p i) n -> p i n", i=PACK))
+
+        def side_by_side(copy, dst, src, lo, hi):
+            copy(
+                out=dst[:, lo:hi, :].rearrange("p (c i) j -> p c j i", i=4),
+                in_=src[:, :, lo:hi].rearrange("p j (c i) -> p c j i", i=4),
+            )
+
+        def quantize_xr(c, a):
+            grouped = stage.tile([P, SPAN, PACK], BF16, name="grouped", align_bytes=64)
+            side_by_side(nc.vector.tensor_copy, grouped, xr_raw[c, a], 0, VCOLS)
+            side_by_side(nc.scalar.copy, grouped, xr_raw[c, a], VCOLS, SPAN)
+            nc.vector.quantize_mx(
+                out=xr_codes[c, a][:].bitcast(FP8X4),
+                scales=xr_scale[c, a][:],
+                in_=grouped[:].rearrange("p t j -> p (t j)"),
+            )
+
+        def mx_pass(c, b, a, rhs, rhs_scale, start, stop):
+            nc.tensor.matmul_mx(
+                out=sum_bank(c, b)[:],
+                lhsT=w_codes[:, a, 2 * P * b : 2 * P * (b + 1)].bitcast(FP4X4),
+                lhsT_scale=w_scale[:, a, P * b : P * (b + 1)],
+                rhs=rhs,
+                rhs_scale=rhs_scale,
+                start=start,
+                stop=stop,
+            )
+
+        def x4_passes(c, tiles):
+            for b in tiles:
+                for a in range(PASSES):
+                    mx_pass(
+                        c, b, a,
+                        x4_codes[:, a, 2 * SPAN * c : 2 * SPAN * (c + 1)].bitcast(FP4X4),
+                        x4_scale[:, a, SPAN * c : SPAN * (c + 1)],
+                        a == 0, False,
+                    )
+
+        def xr_passes(c, a):
+            for b in range(NT):
+                mx_pass(c, b, a, xr_codes[c, a][:].bitcast(FP8X4), xr_scale[c, a][:], False, a == PASSES - 1)
+
+        def drain(c, tiles):
+            for b in tiles:
+                nc.scalar.copy(out=y_t[c, b][:], in_=sum_bank(c, b)[:].rearrange("n (p i) -> n i p", i=PACK))
+
+        def turn(c, tiles):
+            for b in tiles:
+                for i in range(PACK):
+                    nc.tensor.transpose(turn_bank(c, b)[:, P * i : P * (i + 1)], y_t[c, b][:, i, :], ident[:])
+
+        def gate(c, tiles):
+            for b in tiles:
+                cols = slice(P * b, P * (b + 1))
+                nc.vector.tensor_tensor(
+                    out=res[c][:, :, cols],
+                    in0=turn_bank(c, b)[:].rearrange("p (i n) -> p i n", i=PACK),
+                    in1=g_sb[c][:, :, cols],
+                    op=mybir.AluOpType.mult,
+                )
+
+        def round_result(copy, c, tiles):
+            for b in tiles:
+                side_by_side(copy, res_bf[c], res[c], P * b, P * (b + 1))
+
+        def quantize_result(c):
+            nc.vector.quantize_mx(
+                out=res_codes[c][:].bitcast(FP8X4),
+                scales=res_scale[:, c, :],
+                in_=res_bf[c][:].rearrange("p n i -> p (n i)"),
+            )
+
+        def store_result(c):
+            rows = out_0[c * SPAN : (c + 1) * SPAN, :]
+            nc.sync.dma_start(out=rows.rearrange("(p i) n -> p i n", i=PACK), in_=res[c][:])
+
+        def store_codes(c):
+            nc.sync.dma_start(
+                out=out_1[c].rearrange("p n i -> p (n i)").bitcast(I32), in_=res_codes[c][:].bitcast(I32)
+            )
+
+        every, first, second = range(NT), range(NT // 2), range(NT // 2, NT)
+
+        x4_passes(0, every)
+        x4_passes(1, every)
+        for a in range(PASSES):
+            quantize_xr(0, a)
+            xr_passes(0, a)
+        quantize_xr(1, 0)
+        xr_passes(1, 0)
+        drain(0, first)
+        x4_passes(2, first)
+        quantize_xr(1, 1)
+        xr_passes(1, 1)
+        drain(0, second)
+        x4_passes(2, second)
+        quantize_xr(1, 2)
+        xr_passes(1, 2)
+        quantize_xr(2, 0)
+        xr_passes(2, 0)
+        drain(1, first)
+        turn(0, first)
+        quantize_xr(2, 1)
+        xr_passes(2, 1)
+        drain(1, second)
+        turn(0, second)
+        quantize_xr(2, 2)
+        xr_passes(2, 2)
+        drain(2, every)
+
+        gate(0, every)
+        store_result(0)
+        round_result(nc.scalar.copy, 0, every)
+        turn(1, every)
+        gate(1, every)
+        store_result(1)
+        round_result(nc.scalar.copy, 1, every)
+        turn(2, every)
+        gate(2, first)
+        quantize_result(0)
+        store_codes(0)
+        gate(2, second)
+        quantize_result(1)
+        store_codes(1)
+        store_result(2)
+        round_result(nc.scalar.copy, 2, [NT - 1])
+        round_result(nc.vector.tensor_copy, 2, range(NT - 1))
+        quantize_result(2)
+        by_r = out_2.rearrange("a (q r) n -> r q a n", r=4)
+        for r in range(4):
+            nc.sync.dma_start(out=by_r[r].bitcast(I32), in_=res_scale[:].bitcast(I32)[r:P:32])
+        store_codes(2)

@@ -1,7 +1,6 @@
 from contextlib import ExitStack
 
 import concourse.mybir as mybir
-from concourse.masks import make_identity
 
 K, M, T = 1536, 512, 1536
 FLOPS = 2 * 2 * K * M * T
@@ -19,8 +18,7 @@ PACK = 4
 SPAN = P * PACK
 PASSES = K // SPAN
 CHUNKS = T // SPAN
-NT = M // P
-VCOLS = 352
+V_SHARE = 40
 
 
 def tile_mix_xres_tm_pl_mul_kernel(
@@ -38,175 +36,175 @@ def tile_mix_xres_tm_pl_mul_kernel(
 
         w_codes = kept("w_codes", [P, PASSES, 2 * M], U8)
         w_scale = kept("w_scale", [P, PASSES, M], U8)
-        x4_codes = kept("x4_codes", [P, PASSES, 2 * T], U8)
-        x4_scale = kept("x4_scale", [P, PASSES, T], U8)
-        ident = kept("ident", [P, P], F32)
+        x4_codes_in = kept("x4_codes_in", [P, PASSES, 2 * T], U8)
+        x4_scale_in = kept("x4_scale_in", [P, PASSES, T], U8)
+        x4_codes = [kept("x4_codes%d" % c, [P, PASSES, PACK, 2 * P], U8) for c in range(CHUNKS)]
+        x4_scale = [kept("x4_scale%d" % c, [P, PACK, PASSES, P], U8) for c in range(CHUNKS)]
         pieces = [(c, a) for c in range(CHUNKS) for a in range(PASSES)]
         xr_raw = {ca: kept("xr_raw%d%d" % ca, [P, PACK, SPAN], F32) for ca in pieces}
-        xr_codes = {ca: kept("xr_codes%d%d" % ca, [P, SPAN], U32) for ca in pieces}
-        xr_scale = {ca: kept("xr_scale%d%d" % ca, [P, SPAN], U8) for ca in pieces}
+        xr_codes = {ca: kept("xr_codes%d%d" % ca, [P, PACK, P], U32) for ca in pieces}
+        xr_scale = {ca: kept("xr_scale%d%d" % ca, [P, PACK, P], U8) for ca in pieces}
         g_sb = [kept("g_sb%d" % c, [P, PACK, M], F32) for c in range(CHUNKS)]
-        y_t = {(c, b): kept("y_t%d%d" % (c, b), [P, PACK, P], F32) for c in range(CHUNKS) for b in range(NT)}
         res = [kept("res%d" % c, [P, PACK, M], F32) for c in range(CHUNKS)]
         res_bf = [kept("res_bf%d" % c, [P, M, PACK], BF16) for c in range(CHUNKS)]
-        res_codes = [kept("res_codes%d" % c, [P, M], U32) for c in range(CHUNKS)]
+        res_codes = kept("res_codes", [P, CHUNKS, M], U32)
         res_scale = kept("res_scale", [P, CHUNKS, M], U8)
-        banks = [psum.tile([P, SPAN], F32, name="bank%d" % i) for i in range(2 * NT)]
+        banks = [psum.tile([P, M], F32, name="bank%d" % i) for i in range(2 * PACK)]
 
-        def sum_bank(c, b):
-            return banks[NT * (c % 2) + b]
+        def sum_bank(c, r):
+            return banks[PACK * (c % 2) + r]
 
-        def turn_bank(c, b):
-            return banks[(0 if c == CHUNKS - 1 else NT) + b]
-
-        nc.vector.memset(x4_scale[:].bitcast(I32), 0)
+        nc.vector.memset(x4_scale_in[:].bitcast(I32), 0)
         nc.vector.memset(w_scale[:].bitcast(I32), 0)
-        make_identity(nc, ident[:])
 
         def load_scales(plane, rows):
-            by_r = rows.rearrange("a (q r) n -> r q a n", r=4)
-            for r in range(4):
-                nc.sync.dma_start(out=plane[:].bitcast(I32)[r:P:32], in_=by_r[r].bitcast(I32))
+            by_row = rows.rearrange("a (q s) n -> s q a n", s=4)
+            for s in range(4):
+                nc.sync.dma_start(out=plane[:].bitcast(I32)[s:P:32], in_=by_row[s].bitcast(I32))
 
-        nc.sync.dma_start(out=w_codes[:].bitcast(I32), in_=w4_words.rearrange("a p c -> p a c").bitcast(I32))
-        load_scales(x4_scale, x4_scales)
-        nc.sync.dma_start(out=x4_codes[:].bitcast(I32), in_=x4_words.rearrange("a p c -> p a c").bitcast(I32))
-        load_scales(w_scale, w4_scales)
-        for c, a in pieces:
+        def load_xr(c, a):
             rows = xr[a * SPAN : (a + 1) * SPAN, c * SPAN : (c + 1) * SPAN]
             nc.sync.dma_start(out=xr_raw[c, a][:], in_=rows.rearrange("(p j) t -> p j t", j=PACK))
-        for c in range(CHUNKS):
-            rows = g[c * SPAN : (c + 1) * SPAN, :]
-            nc.sync.dma_start(out=g_sb[c][:], in_=rows.rearrange("(p i) n -> p i n", i=PACK))
 
-        def side_by_side(copy, dst, src, lo, hi):
-            copy(
-                out=dst[:, lo:hi, :].rearrange("p (c i) j -> p c j i", i=4),
-                in_=src[:, :, lo:hi].rearrange("p j (c i) -> p c j i", i=4),
+        def load_g(c):
+            rows = g[c * SPAN : (c + 1) * SPAN, :]
+            nc.sync.dma_start(out=g_sb[c][:], in_=rows.rearrange("(p r) n -> p r n", r=PACK))
+
+        nc.sync.dma_start(out=x4_codes_in[:].bitcast(I32), in_=x4_words.rearrange("a p c -> p a c").bitcast(I32))
+        load_scales(x4_scale_in, x4_scales)
+        nc.sync.dma_start(out=w_codes[:].bitcast(I32), in_=w4_words.rearrange("a p c -> p a c").bitcast(I32))
+        load_scales(w_scale, w4_scales)
+        for a in range(PASSES):
+            load_xr(0, a)
+        load_g(0)
+        for c in range(1, CHUNKS):
+            for a in range(PASSES):
+                load_xr(c, a)
+        for c in range(1, CHUNKS):
+            load_g(c)
+
+        def deal_x4_codes(c, a):
+            nc.vector.tensor_copy(
+                out=x4_codes[c][:, a].rearrange("p r (m e) -> p r m e", e=2),
+                in_=x4_codes_in[:, a, 2 * SPAN * c : 2 * SPAN * (c + 1)].rearrange(
+                    "p (m r e) -> p r m e", r=PACK, e=2
+                ),
+            )
+
+        def deal_x4_scale(c):
+            nc.vector.tensor_copy(
+                out=x4_scale[c][:],
+                in_=x4_scale_in[:, :, SPAN * c : SPAN * (c + 1)].rearrange("p a (m r) -> p r a m", r=PACK),
             )
 
         def quantize_xr(c, a):
-            grouped = stage.tile([P, SPAN, PACK], BF16, name="grouped", align_bytes=64)
-            side_by_side(nc.vector.tensor_copy, grouped, xr_raw[c, a], 0, VCOLS)
-            side_by_side(nc.scalar.copy, grouped, xr_raw[c, a], VCOLS, SPAN)
+            grouped = stage.tile([P, PACK, P, PACK], BF16, name="grouped", align_bytes=64)
+            dst = grouped[:].rearrange("p r m j -> p m j r")
+            src = xr_raw[c, a][:].rearrange("p j (m r) -> p m j r", r=PACK)
+            nc.vector.tensor_copy(out=dst[:, :V_SHARE], in_=src[:, :V_SHARE])
+            nc.scalar.copy(out=dst[:, V_SHARE:], in_=src[:, V_SHARE:])
             nc.vector.quantize_mx(
-                out=xr_codes[c, a][:].bitcast(FP8X4),
-                scales=xr_scale[c, a][:],
-                in_=grouped[:].rearrange("p t j -> p (t j)"),
+                out=xr_codes[c, a][:].rearrange("p r m -> p (r m)").bitcast(FP8X4),
+                scales=xr_scale[c, a][:].rearrange("p r m -> p (r m)"),
+                in_=grouped[:].rearrange("p r m j -> p (r m j)"),
             )
 
-        def mx_pass(c, b, a, rhs, rhs_scale, start, stop):
+        def mx_pass(c, r, a, lhsT, lhsT_scale, start, stop):
             nc.tensor.matmul_mx(
-                out=sum_bank(c, b)[:],
-                lhsT=w_codes[:, a, 2 * P * b : 2 * P * (b + 1)].bitcast(FP4X4),
-                lhsT_scale=w_scale[:, a, P * b : P * (b + 1)],
-                rhs=rhs,
-                rhs_scale=rhs_scale,
+                out=sum_bank(c, r)[:],
+                lhsT=lhsT,
+                lhsT_scale=lhsT_scale,
+                rhs=w_codes[:, a, :].bitcast(FP4X4),
+                rhs_scale=w_scale[:, a, :],
                 start=start,
                 stop=stop,
             )
 
-        def x4_passes(c, tiles):
-            for b in tiles:
+        def x4_passes(c, slots):
+            for r in slots:
                 for a in range(PASSES):
-                    mx_pass(
-                        c, b, a,
-                        x4_codes[:, a, 2 * SPAN * c : 2 * SPAN * (c + 1)].bitcast(FP4X4),
-                        x4_scale[:, a, SPAN * c : SPAN * (c + 1)],
-                        a == 0, False,
-                    )
+                    mx_pass(c, r, a, x4_codes[c][:, a, r, :].bitcast(FP4X4), x4_scale[c][:, r, a, :], a == 0, False)
 
         def xr_passes(c, a):
-            for b in range(NT):
-                mx_pass(c, b, a, xr_codes[c, a][:].bitcast(FP8X4), xr_scale[c, a][:], False, a == PASSES - 1)
-
-        def drain(c, tiles):
-            for b in tiles:
-                nc.scalar.copy(out=y_t[c, b][:], in_=sum_bank(c, b)[:].rearrange("n (p i) -> n i p", i=PACK))
-
-        def turn(c, tiles):
-            for b in tiles:
-                for i in range(PACK):
-                    nc.tensor.transpose(turn_bank(c, b)[:, P * i : P * (i + 1)], y_t[c, b][:, i, :], ident[:])
-
-        def gate(c, tiles):
-            for b in tiles:
-                cols = slice(P * b, P * (b + 1))
-                nc.vector.tensor_tensor(
-                    out=res[c][:, :, cols],
-                    in0=turn_bank(c, b)[:].rearrange("p (i n) -> p i n", i=PACK),
-                    in1=g_sb[c][:, :, cols],
-                    op=mybir.AluOpType.mult,
+            for r in range(PACK):
+                mx_pass(
+                    c, r, a, xr_codes[c, a][:, r, :].bitcast(FP8X4), xr_scale[c, a][:, r, :], False, a == PASSES - 1
                 )
 
-        def round_result(copy, c, tiles):
-            for b in tiles:
-                side_by_side(copy, res_bf[c], res[c], P * b, P * (b + 1))
+        def gate(c):
+            for r in range(PACK):
+                nc.vector.tensor_tensor(
+                    out=res[c][:, r, :], in0=sum_bank(c, r)[:], in1=g_sb[c][:, r, :], op=mybir.AluOpType.mult
+                )
+
+        def round_result(copy, c, lo, hi):
+            copy(
+                out=res_bf[c][:, lo:hi, :].rearrange("p (u v) r -> p u r v", v=4),
+                in_=res[c][:, :, lo:hi].rearrange("p r (u v) -> p u r v", v=4),
+            )
 
         def quantize_result(c):
             nc.vector.quantize_mx(
-                out=res_codes[c][:].bitcast(FP8X4),
+                out=res_codes[:, c, :].bitcast(FP8X4),
                 scales=res_scale[:, c, :],
-                in_=res_bf[c][:].rearrange("p n i -> p (n i)"),
+                in_=res_bf[c][:].rearrange("p n r -> p (n r)"),
             )
 
         def store_result(c):
             rows = out_0[c * SPAN : (c + 1) * SPAN, :]
-            nc.sync.dma_start(out=rows.rearrange("(p i) n -> p i n", i=PACK), in_=res[c][:])
+            nc.sync.dma_start(out=rows.rearrange("(p r) n -> p r n", r=PACK), in_=res[c][:])
 
-        def store_codes(c):
-            nc.sync.dma_start(
-                out=out_1[c].rearrange("p n i -> p (n i)").bitcast(I32), in_=res_codes[c][:].bitcast(I32)
-            )
+        every, first, second = range(PACK), range(PACK // 2), range(PACK // 2, PACK)
 
-        every, first, second = range(NT), range(NT // 2), range(NT // 2, NT)
-
+        for c in range(2):
+            for a in range(PASSES):
+                deal_x4_codes(c, a)
+            deal_x4_scale(c)
         x4_passes(0, every)
-        x4_passes(1, every)
-        for a in range(PASSES):
-            quantize_xr(0, a)
-            xr_passes(0, a)
+        quantize_xr(0, 0)
+        xr_passes(0, 0)
+        deal_x4_codes(2, 0)
+        quantize_xr(0, 1)
+        xr_passes(0, 1)
+        x4_passes(1, first)
+        deal_x4_codes(2, 1)
+        quantize_xr(0, 2)
+        xr_passes(0, 2)
+        x4_passes(1, second)
+        deal_x4_codes(2, 2)
+        deal_x4_scale(2)
+        gate(0)
+        x4_passes(2, first)
         quantize_xr(1, 0)
         xr_passes(1, 0)
-        drain(0, first)
-        x4_passes(2, first)
+        round_result(nc.scalar.copy, 0, 0, M // 2)
+        x4_passes(2, second)
         quantize_xr(1, 1)
         xr_passes(1, 1)
-        drain(0, second)
-        x4_passes(2, second)
+        round_result(nc.scalar.copy, 0, M // 2, M)
         quantize_xr(1, 2)
         xr_passes(1, 2)
         quantize_xr(2, 0)
         xr_passes(2, 0)
-        drain(1, first)
-        turn(0, first)
+        quantize_result(0)
         quantize_xr(2, 1)
         xr_passes(2, 1)
-        drain(1, second)
-        turn(0, second)
         quantize_xr(2, 2)
         xr_passes(2, 2)
-        drain(2, every)
-
-        gate(0, every)
         store_result(0)
-        round_result(nc.scalar.copy, 0, every)
-        turn(1, every)
-        gate(1, every)
+
+        gate(1)
         store_result(1)
-        round_result(nc.scalar.copy, 1, every)
-        turn(2, every)
-        gate(2, first)
-        quantize_result(0)
-        store_codes(0)
-        gate(2, second)
-        quantize_result(1)
-        store_codes(1)
+        round_result(nc.scalar.copy, 1, 0, M)
+        gate(2)
         store_result(2)
-        round_result(nc.scalar.copy, 2, [NT - 1])
-        round_result(nc.vector.tensor_copy, 2, range(NT - 1))
+        round_result(nc.vector.tensor_copy, 2, 0, 384)
+        round_result(nc.scalar.copy, 2, 384, M)
+        quantize_result(1)
         quantize_result(2)
-        by_r = out_2.rearrange("a (q r) n -> r q a n", r=4)
-        for r in range(4):
-            nc.sync.dma_start(out=by_r[r].bitcast(I32), in_=res_scale[:].bitcast(I32)[r:P:32])
-        store_codes(2)
+        by_row = out_2.rearrange("a (q s) n -> s q a n", s=4)
+        for s in range(4):
+            nc.sync.dma_start(out=by_row[s].bitcast(I32), in_=res_scale[:].bitcast(I32)[s:P:32])
+        nc.sync.dma_start(
+            out=out_1.rearrange("a p n r -> p a (n r)").bitcast(I32), in_=res_codes[:].bitcast(I32)
+        )

@@ -18,7 +18,7 @@ PACK = 4
 SPAN = P * PACK
 PASSES = K // SPAN
 CHUNKS = T // SPAN
-V_SHARE = 40
+V_EVEN, V_URGENT, V_BUSY = 64, 84, 16
 
 
 def tile_mix_xres_tm_pl_mul_kernel(
@@ -41,7 +41,8 @@ def tile_mix_xres_tm_pl_mul_kernel(
         x4_codes = [kept("x4_codes%d" % c, [P, PASSES, PACK, 2 * P], U8) for c in range(CHUNKS)]
         x4_scale = [kept("x4_scale%d" % c, [P, PACK, PASSES, P], U8) for c in range(CHUNKS)]
         pieces = [(c, a) for c in range(CHUNKS) for a in range(PASSES)]
-        xr_raw = {ca: kept("xr_raw%d%d" % ca, [P, PACK, SPAN], F32) for ca in pieces}
+        xr_wide = [kept("xr_wide%d" % a, [P, PACK, T], F32) for a in range(PASSES - 1)]
+        xr_last = [kept("xr_last%d" % c, [P, PACK, SPAN], F32) for c in range(CHUNKS)]
         xr_codes = {ca: kept("xr_codes%d%d" % ca, [P, PACK, P], U32) for ca in pieces}
         xr_scale = {ca: kept("xr_scale%d%d" % ca, [P, PACK, P], U8) for ca in pieces}
         g_sb = [kept("g_sb%d" % c, [P, PACK, M], F32) for c in range(CHUNKS)]
@@ -62,9 +63,12 @@ def tile_mix_xres_tm_pl_mul_kernel(
             for s in range(4):
                 nc.sync.dma_start(out=plane[:].bitcast(I32)[s:P:32], in_=by_row[s].bitcast(I32))
 
-        def load_xr(c, a):
-            rows = xr[a * SPAN : (a + 1) * SPAN, c * SPAN : (c + 1) * SPAN]
-            nc.sync.dma_start(out=xr_raw[c, a][:], in_=rows.rearrange("(p j) t -> p j t", j=PACK))
+        def load_xr(dst, a, cols):
+            rows = xr[a * SPAN : (a + 1) * SPAN, cols]
+            nc.sync.dma_start(out=dst[:], in_=rows.rearrange("(p j) t -> p j t", j=PACK))
+
+        def load_xr_last(c):
+            load_xr(xr_last[c], PASSES - 1, slice(c * SPAN, (c + 1) * SPAN))
 
         def load_g(c):
             rows = g[c * SPAN : (c + 1) * SPAN, :]
@@ -74,14 +78,14 @@ def tile_mix_xres_tm_pl_mul_kernel(
         load_scales(x4_scale_in, x4_scales)
         nc.sync.dma_start(out=w_codes[:].bitcast(I32), in_=w4_words.rearrange("a p c -> p a c").bitcast(I32))
         load_scales(w_scale, w4_scales)
-        for a in range(PASSES):
-            load_xr(0, a)
+        for a in range(PASSES - 1):
+            load_xr(xr_wide[a], a, slice(0, T))
+        load_xr_last(0)
         load_g(0)
-        for c in range(1, CHUNKS):
-            for a in range(PASSES):
-                load_xr(c, a)
-        for c in range(1, CHUNKS):
-            load_g(c)
+        load_xr_last(1)
+        load_xr_last(2)
+        load_g(1)
+        load_g(2)
 
         def deal_x4_codes(c, a):
             nc.vector.tensor_copy(
@@ -97,12 +101,19 @@ def tile_mix_xres_tm_pl_mul_kernel(
                 in_=x4_scale_in[:, :, SPAN * c : SPAN * (c + 1)].rearrange("p a (m r) -> p r a m", r=PACK),
             )
 
-        def quantize_xr(c, a):
+        xr_bf = {}
+
+        def group_xr(c, a, share):
             grouped = stage.tile([P, PACK, P, PACK], BF16, name="grouped", align_bytes=64)
             dst = grouped[:].rearrange("p r m j -> p m j r")
-            src = xr_raw[c, a][:].rearrange("p j (m r) -> p m j r", r=PACK)
-            nc.vector.tensor_copy(out=dst[:, :V_SHARE], in_=src[:, :V_SHARE])
-            nc.scalar.copy(out=dst[:, V_SHARE:], in_=src[:, V_SHARE:])
+            raw = xr_last[c][:] if a == PASSES - 1 else xr_wide[a][:, :, c * SPAN : (c + 1) * SPAN]
+            src = raw.rearrange("p j (m r) -> p m j r", r=PACK)
+            nc.vector.tensor_copy(out=dst[:, :share], in_=src[:, :share])
+            nc.scalar.copy(out=dst[:, share:], in_=src[:, share:])
+            xr_bf.setdefault((c, a), grouped)
+
+        def quantize_xr(c, a):
+            grouped = xr_bf[c, a]
             nc.vector.quantize_mx(
                 out=xr_codes[c, a][:].rearrange("p r m -> p (r m)").bitcast(FP8X4),
                 scales=xr_scale[c, a][:].rearrange("p r m -> p (r m)"),
@@ -125,14 +136,14 @@ def tile_mix_xres_tm_pl_mul_kernel(
                 for a in range(PASSES):
                     mx_pass(c, r, a, x4_codes[c][:, a, r, :].bitcast(FP4X4), x4_scale[c][:, r, a, :], a == 0, False)
 
-        def xr_passes(c, a):
-            for r in range(PACK):
+        def xr_passes(c, a, slots):
+            for r in slots:
                 mx_pass(
                     c, r, a, xr_codes[c, a][:, r, :].bitcast(FP8X4), xr_scale[c, a][:, r, :], False, a == PASSES - 1
                 )
 
-        def gate(c):
-            for r in range(PACK):
+        def gate(c, slots):
+            for r in slots:
                 nc.vector.tensor_tensor(
                     out=res[c][:, r, :], in0=sum_bank(c, r)[:], in1=g_sb[c][:, r, :], op=mybir.AluOpType.mult
                 )
@@ -150,61 +161,77 @@ def tile_mix_xres_tm_pl_mul_kernel(
                 in_=res_bf[c][:].rearrange("p n r -> p (n r)"),
             )
 
-        def store_result(c):
-            rows = out_0[c * SPAN : (c + 1) * SPAN, :]
-            nc.sync.dma_start(out=rows.rearrange("(p r) n -> p r n", r=PACK), in_=res[c][:])
+        def store_result(c, lo=0, hi=PACK):
+            rows = out_0[c * SPAN : (c + 1) * SPAN, :].rearrange("(p r) n -> p r n", r=PACK)
+            nc.sync.dma_start(out=rows[:, lo:hi, :], in_=res[c][:, lo:hi, :])
+
+        def store_codes(c):
+            nc.sync.dma_start(
+                out=out_1[c].rearrange("p n r -> p (n r)").bitcast(I32), in_=res_codes[:, c, :].bitcast(I32)
+            )
 
         every, first, second = range(PACK), range(PACK // 2), range(PACK // 2, PACK)
 
-        for c in range(2):
+        for c in range(CHUNKS):
             for a in range(PASSES):
                 deal_x4_codes(c, a)
             deal_x4_scale(c)
         x4_passes(0, every)
-        quantize_xr(0, 0)
-        xr_passes(0, 0)
-        deal_x4_codes(2, 0)
-        quantize_xr(0, 1)
-        xr_passes(0, 1)
-        x4_passes(1, first)
-        deal_x4_codes(2, 1)
-        quantize_xr(0, 2)
-        xr_passes(0, 2)
-        x4_passes(1, second)
-        deal_x4_codes(2, 2)
-        deal_x4_scale(2)
-        gate(0)
-        x4_passes(2, first)
-        quantize_xr(1, 0)
-        xr_passes(1, 0)
-        round_result(nc.scalar.copy, 0, 0, M // 2)
-        x4_passes(2, second)
-        quantize_xr(1, 1)
-        xr_passes(1, 1)
-        round_result(nc.scalar.copy, 0, M // 2, M)
-        quantize_xr(1, 2)
-        xr_passes(1, 2)
-        quantize_xr(2, 0)
-        xr_passes(2, 0)
-        quantize_result(0)
-        quantize_xr(2, 1)
-        xr_passes(2, 1)
-        quantize_xr(2, 2)
-        xr_passes(2, 2)
-        store_result(0)
+        x4_passes(1, every)
 
-        gate(1)
-        store_result(1)
+        group_xr(0, 0, V_EVEN)
+        group_xr(1, 0, V_EVEN)
+        quantize_xr(0, 0)
+        group_xr(2, 0, V_EVEN)
+        quantize_xr(1, 0)
+        quantize_xr(2, 0)
+        xr_passes(0, 0, every)
+        xr_passes(1, 0, every)
+
+        group_xr(0, 1, V_URGENT)
+        group_xr(1, 1, V_EVEN)
+        quantize_xr(0, 1)
+        xr_passes(0, 1, every)
+        group_xr(0, 2, V_URGENT)
+        group_xr(2, 1, V_BUSY)
+        quantize_xr(0, 2)
+        quantize_xr(1, 1)
+        xr_passes(0, 2, every)
+        xr_passes(1, 1, every)
+        gate(0, every)
+
+        group_xr(1, 2, V_EVEN)
+        quantize_xr(2, 1)
+        quantize_xr(1, 2)
+        x4_passes(2, first)
+        xr_passes(2, 0, first)
+        xr_passes(2, 1, first)
+        xr_passes(1, 2, every)
+        group_xr(2, 2, V_URGENT)
+        quantize_xr(2, 2)
+        x4_passes(2, second)
+        xr_passes(2, 2, first)
+        for a in range(PASSES):
+            xr_passes(2, a, second)
+
+        round_result(nc.scalar.copy, 0, 0, M)
+        gate(1, every)
         round_result(nc.scalar.copy, 1, 0, M)
-        gate(2)
-        store_result(2)
-        round_result(nc.vector.tensor_copy, 2, 0, 384)
-        round_result(nc.scalar.copy, 2, 384, M)
+        gate(2, first)
+        quantize_result(0)
+        gate(2, second)
+        round_result(nc.scalar.copy, 2, 320, M)
+        round_result(nc.vector.tensor_copy, 2, 0, 320)
         quantize_result(1)
         quantize_result(2)
+
+        store_result(0)
+        store_result(1)
+        store_codes(0)
+        store_result(2, 0, 2)
+        store_result(2, 2, 4)
+        store_codes(1)
         by_row = out_2.rearrange("a (q s) n -> s q a n", s=4)
         for s in range(4):
             nc.sync.dma_start(out=by_row[s].bitcast(I32), in_=res_scale[:].bitcast(I32)[s:P:32])
-        nc.sync.dma_start(
-            out=out_1.rearrange("a p n r -> p a (n r)").bitcast(I32), in_=res_codes[:].bitcast(I32)
-        )
+        store_codes(2)

@@ -75,8 +75,8 @@ def tile_mix_xres_tm_pl_mul_kernel(
             nc.sync.dma_start(out=g_sb[c][:], in_=rows.rearrange("(p r) n -> p r n", r=PACK))
 
         nc.sync.dma_start(out=x4_codes_in[:].bitcast(I32), in_=x4_words.rearrange("a p c -> p a c").bitcast(I32))
-        load_scales(x4_scale_in, x4_scales)
         nc.sync.dma_start(out=w_codes[:].bitcast(I32), in_=w4_words.rearrange("a p c -> p a c").bitcast(I32))
+        load_scales(x4_scale_in, x4_scales)
         load_scales(w_scale, w4_scales)
         for a in range(PASSES - 1):
             load_xr(xr_wide[a], a, slice(0, T))
@@ -172,10 +172,12 @@ def tile_mix_xres_tm_pl_mul_kernel(
 
         every, first, second = range(PACK), range(PACK // 2), range(PACK // 2, PACK)
 
-        for c in range(CHUNKS):
-            for a in range(PASSES):
-                deal_x4_codes(c, a)
-            deal_x4_scale(c)
+        for group in ((0, 1), (2,)):
+            for c in group:
+                for a in range(PASSES):
+                    deal_x4_codes(c, a)
+            for c in group:
+                deal_x4_scale(c)
         x4_passes(0, every)
         x4_passes(1, every)
 
@@ -231,7 +233,7 @@ def tile_mix_xres_tm_pl_mul_kernel(
         store_result(2, 0, 2)
         store_result(2, 2, 4)
         store_codes(1)
+        store_codes(2)
         by_row = out_2.rearrange("a (q s) n -> s q a n", s=4)
         for s in range(4):
             nc.sync.dma_start(out=by_row[s].bitcast(I32), in_=res_scale[:].bitcast(I32)[s:P:32])
-        store_codes(2)

@@ -10,6 +10,7 @@ BF16 = mybir.dt.bfloat16
 I32 = mybir.dt.int32
 U32 = mybir.dt.uint32
 U8 = mybir.dt.uint8
+U16 = mybir.dt.uint16
 FP8X4 = mybir.dt.float8_e4m3fn_x4
 FP4X4 = mybir.dt.float4_e2m1fn_x4
 
@@ -18,7 +19,6 @@ PACK = 4
 SPAN = P * PACK
 PASSES = K // SPAN
 CHUNKS = T // SPAN
-V_EVEN, V_URGENT, V_BUSY = 64, 84, 16
 
 
 def tile_mix_xres_tm_pl_mul_kernel(
@@ -41,12 +41,14 @@ def tile_mix_xres_tm_pl_mul_kernel(
         x4_codes = [kept("x4_codes%d" % c, [P, PASSES, PACK, 2 * P], U8) for c in range(CHUNKS)]
         x4_scale = [kept("x4_scale%d" % c, [P, PACK, PASSES, P], U8) for c in range(CHUNKS)]
         pieces = [(c, a) for c in range(CHUNKS) for a in range(PASSES)]
-        xr_wide = [kept("xr_wide%d" % a, [P, PACK, T], F32) for a in range(PASSES - 1)]
-        xr_last = [kept("xr_last%d" % c, [P, PACK, SPAN], F32) for c in range(CHUNKS)]
+        xr_raw = {}
         xr_codes = {ca: kept("xr_codes%d%d" % ca, [P, PACK, P], U32) for ca in pieces}
         xr_scale = {ca: kept("xr_scale%d%d" % ca, [P, PACK, P], U8) for ca in pieces}
         g_sb = [kept("g_sb%d" % c, [P, PACK, M], F32) for c in range(CHUNKS)]
-        res = [kept("res%d" % c, [P, PACK, M], F32) for c in range(CHUNKS)]
+        res_all = kept("res_all", [P, CHUNKS * PACK * M], F32)
+        res = [
+            res_all[:, c * PACK * M : (c + 1) * PACK * M].rearrange("p (r n) -> p r n", r=PACK) for c in range(CHUNKS)
+        ]
         res_bf = [kept("res_bf%d" % c, [P, M, PACK], BF16) for c in range(CHUNKS)]
         res_codes = kept("res_codes", [P, CHUNKS, M], U32)
         res_scale = kept("res_scale", [P, CHUNKS, M], U8)
@@ -63,36 +65,41 @@ def tile_mix_xres_tm_pl_mul_kernel(
             for s in range(4):
                 nc.sync.dma_start(out=plane[:].bitcast(I32)[s:P:32], in_=by_row[s].bitcast(I32))
 
-        def load_xr(dst, a, cols):
-            rows = xr[a * SPAN : (a + 1) * SPAN, cols]
+        def load_xr(a, lo, hi):
+            dst = kept("xr_raw%d%d" % (a, lo), [P, PACK, (hi - lo) * SPAN], F32)
+            rows = xr[a * SPAN : (a + 1) * SPAN, lo * SPAN : hi * SPAN]
             nc.sync.dma_start(out=dst[:], in_=rows.rearrange("(p j) t -> p j t", j=PACK))
-
-        def load_xr_last(c):
-            load_xr(xr_last[c], PASSES - 1, slice(c * SPAN, (c + 1) * SPAN))
+            for c in range(lo, hi):
+                xr_raw.setdefault((c, a), dst[:, :, (c - lo) * SPAN : (c - lo + 1) * SPAN])
 
         def load_g(c):
             rows = g[c * SPAN : (c + 1) * SPAN, :]
             nc.sync.dma_start(out=g_sb[c][:], in_=rows.rearrange("(p r) n -> p r n", r=PACK))
 
-        nc.sync.dma_start(out=x4_codes_in[:].bitcast(I32), in_=x4_words.rearrange("a p c -> p a c").bitcast(I32))
-        nc.sync.dma_start(out=w_codes[:].bitcast(I32), in_=w4_words.rearrange("a p c -> p a c").bitcast(I32))
+        def load_codes(dst, words):
+            nc.sync.dma_start(out=dst[:].bitcast(I32), in_=words.rearrange("a p c -> p a c").bitcast(I32))
+
+        load_codes(x4_codes_in, x4_words)
         load_scales(x4_scale_in, x4_scales)
+        load_codes(w_codes, w4_words)
         load_scales(w_scale, w4_scales)
-        for a in range(PASSES - 1):
-            load_xr(xr_wide[a], a, slice(0, T))
-        load_xr_last(0)
+        load_xr(0, 0, 1)
+        load_xr(1, 0, 1)
+        load_xr(2, 0, 1)
         load_g(0)
-        load_xr_last(1)
-        load_xr_last(2)
+        load_xr(0, 1, 3)
+        load_xr(1, 1, 3)
+        load_xr(2, 1, 2)
+        load_xr(2, 2, 3)
         load_g(1)
         load_g(2)
 
         def deal_x4_codes(c, a):
             nc.vector.tensor_copy(
-                out=x4_codes[c][:, a].rearrange("p r (m e) -> p r m e", e=2),
-                in_=x4_codes_in[:, a, 2 * SPAN * c : 2 * SPAN * (c + 1)].rearrange(
-                    "p (m r e) -> p r m e", r=PACK, e=2
-                ),
+                out=x4_codes[c][:, a].bitcast(U16),
+                in_=x4_codes_in[:, a, 2 * SPAN * c : 2 * SPAN * (c + 1)]
+                .bitcast(U16)
+                .rearrange("p (m r) -> p r m", r=PACK),
             )
 
         def deal_x4_scale(c):
@@ -106,8 +113,7 @@ def tile_mix_xres_tm_pl_mul_kernel(
         def group_xr(c, a, share):
             grouped = stage.tile([P, PACK, P, PACK], BF16, name="grouped", align_bytes=64)
             dst = grouped[:].rearrange("p r m j -> p m j r")
-            raw = xr_last[c][:] if a == PASSES - 1 else xr_wide[a][:, :, c * SPAN : (c + 1) * SPAN]
-            src = raw.rearrange("p j (m r) -> p m j r", r=PACK)
+            src = xr_raw[c, a].rearrange("p j (m r) -> p m j r", r=PACK)
             nc.vector.tensor_copy(out=dst[:, :share], in_=src[:, :share])
             nc.scalar.copy(out=dst[:, share:], in_=src[:, share:])
             xr_bf.setdefault((c, a), grouped)
@@ -161,79 +167,75 @@ def tile_mix_xres_tm_pl_mul_kernel(
                 in_=res_bf[c][:].rearrange("p n r -> p (n r)"),
             )
 
-        def store_result(c, lo=0, hi=PACK):
-            rows = out_0[c * SPAN : (c + 1) * SPAN, :].rearrange("(p r) n -> p r n", r=PACK)
-            nc.sync.dma_start(out=rows[:, lo:hi, :], in_=res[c][:, lo:hi, :])
+        def store_result(lo, hi):
+            rows = out_0[lo * SPAN : hi * SPAN, :].rearrange("(c p r) n -> p c (r n)", p=P, r=PACK)
+            nc.sync.dma_start(out=rows, in_=res_all[:, lo * PACK * M : hi * PACK * M].rearrange("p (c x) -> p c x", x=PACK * M))
 
-        def store_codes(c):
+        def store_codes(lo, hi):
             nc.sync.dma_start(
-                out=out_1[c].rearrange("p n r -> p (n r)").bitcast(I32), in_=res_codes[:, c, :].bitcast(I32)
+                out=out_1[lo:hi].rearrange("c p n r -> p c (n r)").bitcast(I32), in_=res_codes[:, lo:hi, :].bitcast(I32)
             )
 
-        every, first, second = range(PACK), range(PACK // 2), range(PACK // 2, PACK)
+        every = range(PACK)
 
-        for group in ((0, 1), (2,)):
-            for c in group:
-                for a in range(PASSES):
-                    deal_x4_codes(c, a)
-            for c in group:
-                deal_x4_scale(c)
+        for a in range(PASSES):
+            deal_x4_codes(0, a)
+        for a in range(PASSES):
+            deal_x4_codes(1, a)
+        deal_x4_scale(0)
         x4_passes(0, every)
-        x4_passes(1, every)
-
-        group_xr(0, 0, V_EVEN)
-        group_xr(1, 0, V_EVEN)
+        deal_x4_scale(1)
+        x4_passes(1, range(0, 1))
+        for a in range(PASSES):
+            deal_x4_codes(2, a)
+        deal_x4_scale(2)
+        group_xr(0, 0, 32)
         quantize_xr(0, 0)
-        group_xr(2, 0, V_EVEN)
-        quantize_xr(1, 0)
-        quantize_xr(2, 0)
         xr_passes(0, 0, every)
-        xr_passes(1, 0, every)
-
-        group_xr(0, 1, V_URGENT)
-        group_xr(1, 1, V_EVEN)
+        x4_passes(1, range(1, 2))
+        group_xr(0, 1, 64)
         quantize_xr(0, 1)
         xr_passes(0, 1, every)
-        group_xr(0, 2, V_URGENT)
-        group_xr(2, 1, V_BUSY)
+        group_xr(0, 2, 84)
         quantize_xr(0, 2)
-        quantize_xr(1, 1)
         xr_passes(0, 2, every)
-        xr_passes(1, 1, every)
+        x4_passes(1, range(2, 4))
         gate(0, every)
-
-        group_xr(1, 2, V_EVEN)
-        quantize_xr(2, 1)
-        quantize_xr(1, 2)
-        x4_passes(2, first)
-        xr_passes(2, 0, first)
-        xr_passes(2, 1, first)
-        xr_passes(1, 2, every)
-        group_xr(2, 2, V_URGENT)
-        quantize_xr(2, 2)
-        x4_passes(2, second)
-        xr_passes(2, 2, first)
-        for a in range(PASSES):
-            xr_passes(2, a, second)
-
-        round_result(nc.scalar.copy, 0, 0, M)
-        gate(1, every)
-        round_result(nc.scalar.copy, 1, 0, M)
-        gate(2, first)
+        x4_passes(2, every)
+        round_result(nc.scalar.copy, 0, 320, 512)
+        round_result(nc.vector.tensor_copy, 0, 0, 320)
+        group_xr(1, 0, 64)
         quantize_result(0)
-        gate(2, second)
-        round_result(nc.scalar.copy, 2, 320, M)
-        round_result(nc.vector.tensor_copy, 2, 0, 320)
+        group_xr(2, 0, 64)
+        quantize_xr(1, 0)
+        xr_passes(1, 0, every)
+        quantize_xr(2, 0)
+        xr_passes(2, 0, every)
+        group_xr(1, 1, 64)
+        group_xr(2, 1, 64)
+        quantize_xr(1, 1)
+        xr_passes(1, 1, every)
+        group_xr(1, 2, 64)
+        quantize_xr(2, 1)
+        xr_passes(2, 1, every)
+        quantize_xr(1, 2)
+        xr_passes(1, 2, every)
+        group_xr(2, 2, 64)
+        quantize_xr(2, 2)
+        xr_passes(2, 2, every)
+        gate(1, every)
+        round_result(nc.scalar.copy, 1, 0, 512)
+        gate(2, every)
+        round_result(nc.scalar.copy, 2, 384, 512)
+        round_result(nc.vector.tensor_copy, 2, 0, 384)
         quantize_result(1)
         quantize_result(2)
 
-        store_result(0)
-        store_result(1)
-        store_codes(0)
-        store_result(2, 0, 2)
-        store_result(2, 2, 4)
-        store_codes(1)
-        store_codes(2)
+        store_result(0, 1)
+        store_codes(0, 1)
+        store_result(1, 2)
+        store_result(2, 3)
+        store_codes(1, 3)
         by_row = out_2.rearrange("a (q s) n -> s q a n", s=4)
         for s in range(4):
             nc.sync.dma_start(out=by_row[s].bitcast(I32), in_=res_scale[:].bitcast(I32)[s:P:32])

@@ -32,7 +32,7 @@ def tile_mix_xres_tm_pl_mul_kernel(
         ctx.enter_context(tc.manual_schedule())
 
         def kept(name, shape, dtype):
-            return keep.tile(shape, dtype, name=name, align_bytes=64)
+            return keep.tile(shape, dtype, name=name, align_bytes=256)
 
         w_codes = kept("w_codes", [P, PASSES, 2 * M], U8)
         w_scale = kept("w_scale", [P, PASSES, M], U8)

@@ -27,7 +27,7 @@ def tile_mix_xres_tm_pl_mul_kernel(
     nc = tc.nc
     with ExitStack() as ctx:
         keep = ctx.enter_context(tc.tile_pool(name="keep", bufs=1))
-        stage = ctx.enter_context(tc.tile_pool(name="stage", bufs=3))
+        stage = ctx.enter_context(tc.tile_pool(name="stage", bufs=4))
         psum = ctx.enter_context(tc.psum_pool(name="psum", bufs=1))
         ctx.enter_context(tc.manual_schedule())
 
@@ -57,13 +57,13 @@ def tile_mix_xres_tm_pl_mul_kernel(
         def sum_bank(c, r):
             return banks[PACK * (c % 2) + r]
 
-        nc.vector.memset(x4_scale_in[:].bitcast(I32), 0)
         nc.vector.memset(w_scale[:].bitcast(I32), 0)
+        nc.vector.memset(x4_scale_in[:].bitcast(I32), 0)
 
-        def load_scales(plane, rows):
+        def load_scales(plane, rows, queue):
             by_row = rows.rearrange("a (q s) n -> s q a n", s=4)
             for s in range(4):
-                nc.sync.dma_start(out=plane[:].bitcast(I32)[s:P:32], in_=by_row[s].bitcast(I32))
+                queue.dma_start(out=plane[:].bitcast(I32)[s:P:32], in_=by_row[s].bitcast(I32))
 
         def load_xr(a, lo, hi):
             dst = kept("xr_raw%d%d" % (a, lo), [P, PACK, (hi - lo) * SPAN], F32)
@@ -80,9 +80,9 @@ def tile_mix_xres_tm_pl_mul_kernel(
             nc.sync.dma_start(out=dst[:].bitcast(I32), in_=words.rearrange("a p c -> p a c").bitcast(I32))
 
         load_codes(x4_codes_in, x4_words)
-        load_scales(x4_scale_in, x4_scales)
+        load_scales(w_scale, w4_scales, nc.sync)
+        load_scales(x4_scale_in, x4_scales, nc.scalar)
         load_codes(w_codes, w4_words)
-        load_scales(w_scale, w4_scales)
         load_xr(0, 0, 1)
         load_xr(1, 0, 1)
         load_xr(2, 0, 1)
@@ -109,14 +109,18 @@ def tile_mix_xres_tm_pl_mul_kernel(
             )
 
         xr_bf = {}
+        on_vector, on_scalar = nc.vector.tensor_copy, nc.scalar.copy
+
+        def group_part(copy, c, a, lo, hi):
+            if (c, a) not in xr_bf:
+                xr_bf.setdefault((c, a), stage.tile([P, PACK, P, PACK], BF16, name="grouped", align_bytes=256))
+            dst = xr_bf[c, a][:].rearrange("p r m j -> p m j r")
+            src = xr_raw[c, a].rearrange("p j (m r) -> p m j r", r=PACK)
+            copy(out=dst[:, lo:hi], in_=src[:, lo:hi])
 
         def group_xr(c, a, share):
-            grouped = stage.tile([P, PACK, P, PACK], BF16, name="grouped", align_bytes=64)
-            dst = grouped[:].rearrange("p r m j -> p m j r")
-            src = xr_raw[c, a].rearrange("p j (m r) -> p m j r", r=PACK)
-            nc.vector.tensor_copy(out=dst[:, :share], in_=src[:, :share])
-            nc.scalar.copy(out=dst[:, share:], in_=src[:, share:])
-            xr_bf.setdefault((c, a), grouped)
+            group_part(on_vector, c, a, 0, share)
+            group_part(on_scalar, c, a, share, P)
 
         def quantize_xr(c, a):
             grouped = xr_bf[c, a]
@@ -126,27 +130,29 @@ def tile_mix_xres_tm_pl_mul_kernel(
                 in_=grouped[:].rearrange("p r m j -> p (r m j)"),
             )
 
-        def mx_pass(c, r, a, lhsT, lhsT_scale, start, stop):
+        passes_done = {}
+
+        def mx_pass(c, r, a, lhsT, lhsT_scale):
+            done = passes_done.setdefault((c, r), [])
+            done.append(a)
             nc.tensor.matmul_mx(
                 out=sum_bank(c, r)[:],
                 lhsT=lhsT,
                 lhsT_scale=lhsT_scale,
                 rhs=w_codes[:, a, :].bitcast(FP4X4),
                 rhs_scale=w_scale[:, a, :],
-                start=start,
-                stop=stop,
+                start=len(done) == 1,
+                stop=len(done) == 2 * PASSES,
             )
 
         def x4_passes(c, slots):
             for r in slots:
                 for a in range(PASSES):
-                    mx_pass(c, r, a, x4_codes[c][:, a, r, :].bitcast(FP4X4), x4_scale[c][:, r, a, :], a == 0, False)
+                    mx_pass(c, r, a, x4_codes[c][:, a, r, :].bitcast(FP4X4), x4_scale[c][:, r, a, :])
 
         def xr_passes(c, a, slots):
             for r in slots:
-                mx_pass(
-                    c, r, a, xr_codes[c, a][:, r, :].bitcast(FP8X4), xr_scale[c, a][:, r, :], False, a == PASSES - 1
-                )
+                mx_pass(c, r, a, xr_codes[c, a][:, r, :].bitcast(FP8X4), xr_scale[c, a][:, r, :])
 
         def gate(c, slots):
             for r in slots:
@@ -178,32 +184,26 @@ def tile_mix_xres_tm_pl_mul_kernel(
 
         every = range(PACK)
 
-        for a in range(PASSES):
-            deal_x4_codes(0, a)
-        for a in range(PASSES):
-            deal_x4_codes(1, a)
-        deal_x4_scale(0)
-        x4_passes(0, every)
-        deal_x4_scale(1)
-        x4_passes(1, range(0, 1))
-        for a in range(PASSES):
-            deal_x4_codes(2, a)
-        deal_x4_scale(2)
-        group_xr(0, 0, 32)
+        share = 64
+
+        for c in range(CHUNKS):
+            for a in range(PASSES):
+                deal_x4_codes(c, a)
+        group_xr(0, 0, share)
         quantize_xr(0, 0)
+        deal_x4_scale(0)
         xr_passes(0, 0, every)
-        x4_passes(1, range(1, 2))
-        group_xr(0, 1, 64)
-        quantize_xr(0, 1)
-        xr_passes(0, 1, every)
-        group_xr(0, 2, 84)
-        quantize_xr(0, 2)
-        xr_passes(0, 2, every)
-        x4_passes(1, range(2, 4))
+        x4_passes(0, every)
+        for a in (1, 2):
+            group_xr(0, a, share)
+            deal_x4_scale(a)
+            quantize_xr(0, a)
+            xr_passes(0, a, every)
+        x4_passes(1, every)
         gate(0, every)
         x4_passes(2, every)
-        round_result(nc.scalar.copy, 0, 320, 512)
-        round_result(nc.vector.tensor_copy, 0, 0, 320)
+        round_result(on_scalar, 0, 256, M)
+        round_result(on_vector, 0, 0, 256)
         group_xr(1, 0, 64)
         quantize_result(0)
         group_xr(2, 0, 64)
@@ -224,10 +224,10 @@ def tile_mix_xres_tm_pl_mul_kernel(
         quantize_xr(2, 2)
         xr_passes(2, 2, every)
         gate(1, every)
-        round_result(nc.scalar.copy, 1, 0, 512)
+        round_result(on_scalar, 1, 0, M)
         gate(2, every)
-        round_result(nc.scalar.copy, 2, 384, 512)
-        round_result(nc.vector.tensor_copy, 2, 0, 384)
+        round_result(on_scalar, 2, 384, M)
+        round_result(on_vector, 2, 0, 384)
         quantize_result(1)
         quantize_result(2)
 

@@ -60,9 +60,9 @@ def tile_mix_xres_tm_pl_mul_kernel(
         nc.vector.memset(w_scale[:].bitcast(I32), 0)
         nc.vector.memset(x4_scale_in[:].bitcast(I32), 0)
 
-        def load_scales(plane, rows, queue):
+        def load_scales(plane, rows, queue, lo=0, hi=4):
             by_row = rows.rearrange("a (q s) n -> s q a n", s=4)
-            for s in range(4):
+            for s in range(lo, hi):
                 queue.dma_start(out=plane[:].bitcast(I32)[s:P:32], in_=by_row[s].bitcast(I32))
 
         def load_xr(a, lo, hi):
@@ -80,10 +80,10 @@ def tile_mix_xres_tm_pl_mul_kernel(
             nc.sync.dma_start(out=dst[:].bitcast(I32), in_=words.rearrange("a p c -> p a c").bitcast(I32))
 
         load_codes(x4_codes_in, x4_words)
-        load_scales(w_scale, w4_scales, nc.sync)
-        load_scales(x4_scale_in, x4_scales, nc.scalar)
         load_codes(w_codes, w4_words)
         load_xr(0, 0, 1)
+        load_scales(w_scale, w4_scales, nc.scalar)
+        load_scales(x4_scale_in, x4_scales, nc.scalar)
         load_xr(1, 0, 1)
         load_xr(2, 0, 1)
         load_g(0)
@@ -189,7 +189,7 @@ def tile_mix_xres_tm_pl_mul_kernel(
         for c in range(CHUNKS):
             for a in range(PASSES):
                 deal_x4_codes(c, a)
-        group_xr(0, 0, share)
+        group_part(on_vector, 0, 0, 0, P)
         quantize_xr(0, 0)
         deal_x4_scale(0)
         xr_passes(0, 0, every)

@@ -19,6 +19,7 @@ PACK = 4
 SPAN = P * PACK
 PASSES = K // SPAN
 CHUNKS = T // SPAN
+SCALE_ROW = 4
 
 
 def tile_mix_xres_tm_pl_mul_kernel(
@@ -169,7 +170,7 @@ def tile_mix_xres_tm_pl_mul_kernel(
         def quantize_result(c):
             nc.vector.quantize_mx(
                 out=res_codes[:, c, :].bitcast(FP8X4),
-                scales=res_scale[:, c, :],
+                scales=res_scale[SCALE_ROW:, c, :],
                 in_=res_bf[c][:].rearrange("p n r -> p (n r)"),
             )
 
@@ -238,4 +239,4 @@ def tile_mix_xres_tm_pl_mul_kernel(
         store_codes(1, 3)
         by_row = out_2.rearrange("a (q s) n -> s q a n", s=4)
         for s in range(4):
-            nc.sync.dma_start(out=by_row[s].bitcast(I32), in_=res_scale[:].bitcast(I32)[s:P:32])
+            nc.scalar.dma_start(out=by_row[s].bitcast(I32), in_=res_scale[:].bitcast(I32)[SCALE_ROW + s : P : 32])

@@ -155,10 +155,13 @@ def tile_mix_xres_tm_pl_mul_kernel(
             for r in slots:
                 mx_pass(c, r, a, xr_codes[c, a][:, r, :].bitcast(FP8X4), xr_scale[c, a][:, r, :])
 
-        def gate(c, slots):
+        def gate(c, slots, lo=0, hi=M):
             for r in slots:
                 nc.vector.tensor_tensor(
-                    out=res[c][:, r, :], in0=sum_bank(c, r)[:], in1=g_sb[c][:, r, :], op=mybir.AluOpType.mult
+                    out=res[c][:, r, lo:hi],
+                    in0=sum_bank(c, r)[:, lo:hi],
+                    in1=g_sb[c][:, r, lo:hi],
+                    op=mybir.AluOpType.mult,
                 )
 
         def round_result(copy, c, lo, hi):
@@ -167,16 +170,25 @@ def tile_mix_xres_tm_pl_mul_kernel(
                 in_=res[c][:, :, lo:hi].rearrange("p r (u v) -> p u r v", v=4),
             )
 
-        def quantize_result(c):
+        def quantize_result(c, lo=0, hi=M):
             nc.vector.quantize_mx(
-                out=res_codes[:, c, :].bitcast(FP8X4),
-                scales=res_scale[SCALE_ROW:, c, :],
-                in_=res_bf[c][:].rearrange("p n r -> p (n r)"),
+                out=res_codes[:, c, lo:hi].bitcast(FP8X4),
+                scales=res_scale[SCALE_ROW:, c, lo:hi],
+                in_=res_bf[c][:, lo:hi, :].rearrange("p n r -> p (n r)"),
             )
 
         def store_result(lo, hi):
             rows = out_0[lo * SPAN : hi * SPAN, :].rearrange("(c p r) n -> p c (r n)", p=P, r=PACK)
             nc.sync.dma_start(out=rows, in_=res_all[:, lo * PACK * M : hi * PACK * M].rearrange("p (c x) -> p c x", x=PACK * M))
+
+        def store_slots(c, lo, hi):
+            rows = out_0[c * SPAN : (c + 1) * SPAN, :].rearrange("(p r) n -> p (r n)", r=PACK)
+            first = c * PACK * M
+            nc.sync.dma_start(out=rows[:, lo * M : hi * M], in_=res_all[:, first + lo * M : first + hi * M])
+
+        def store_columns(c, lo, hi):
+            rows = out_0[c * SPAN : (c + 1) * SPAN, lo:hi].rearrange("(p r) n -> p r n", r=PACK)
+            nc.sync.dma_start(out=rows, in_=res[c][:, :, lo:hi])
 
         def store_codes(lo, hi):
             nc.sync.dma_start(
@@ -218,24 +230,30 @@ def tile_mix_xres_tm_pl_mul_kernel(
         xr_passes(1, 1, every)
         group_xr(1, 2, 64)
         quantize_xr(2, 1)
-        xr_passes(2, 1, every)
         quantize_xr(1, 2)
         xr_passes(1, 2, every)
+        xr_passes(2, 1, every)
         group_xr(2, 2, 64)
         quantize_xr(2, 2)
         xr_passes(2, 2, every)
-        gate(1, every)
-        round_result(on_scalar, 1, 0, M)
-        gate(2, every)
-        round_result(on_scalar, 2, 384, M)
-        round_result(on_vector, 2, 0, 384)
+        half = M // 2
+        for c in (1, 2):
+            gate(c, every, 0, half)
+            round_result(on_scalar, c, 0, half)
+            gate(c, every, half, M)
+            if c == 1:
+                round_result(on_scalar, c, half, M)
+        round_result(on_scalar, 2, 416, M)
         quantize_result(1)
-        quantize_result(2)
+        round_result(on_vector, 2, half, 416)
+        quantize_result(2, 0, half)
+        quantize_result(2, half, M)
 
         store_result(0, 1)
         store_codes(0, 1)
-        store_result(1, 2)
-        store_result(2, 3)
+        for c in (1, 2):
+            store_columns(c, 0, half)
+            store_columns(c, half, M)
         store_codes(1, 3)
         by_row = out_2.rearrange("a (q s) n -> s q a n", s=4)
         for s in range(4):

@@ -19,7 +19,14 @@ PACK = 4
 SPAN = P * PACK
 PASSES = K // SPAN
 CHUNKS = T // SPAN
-SCALE_ROW = 4
+QUADRANT = 32
+GROUP_ROWS = 4
+ALIGN = 256
+RESULT_PLANE = 4
+STAGE_BUFS = 4
+HALF = M // 2
+PIECE_SHARE = 72
+LAST_SPLIT = 416
 
 
 def tile_mix_xres_tm_pl_mul_kernel(
@@ -28,12 +35,12 @@ def tile_mix_xres_tm_pl_mul_kernel(
     nc = tc.nc
     with ExitStack() as ctx:
         keep = ctx.enter_context(tc.tile_pool(name="keep", bufs=1))
-        stage = ctx.enter_context(tc.tile_pool(name="stage", bufs=4))
+        stage = ctx.enter_context(tc.tile_pool(name="stage", bufs=STAGE_BUFS))
         psum = ctx.enter_context(tc.psum_pool(name="psum", bufs=1))
         ctx.enter_context(tc.manual_schedule())
 
         def kept(name, shape, dtype):
-            return keep.tile(shape, dtype, name=name, align_bytes=256)
+            return keep.tile(shape, dtype, name=name, align_bytes=ALIGN)
 
         w_codes = kept("w_codes", [P, PASSES, 2 * M], U8)
         w_scale = kept("w_scale", [P, PASSES, M], U8)
@@ -42,7 +49,6 @@ def tile_mix_xres_tm_pl_mul_kernel(
         x4_codes = [kept("x4_codes%d" % c, [P, PASSES, PACK, 2 * P], U8) for c in range(CHUNKS)]
         x4_scale = [kept("x4_scale%d" % c, [P, PACK, PASSES, P], U8) for c in range(CHUNKS)]
         pieces = [(c, a) for c in range(CHUNKS) for a in range(PASSES)]
-        xr_raw = {}
         xr_codes = {ca: kept("xr_codes%d%d" % ca, [P, PACK, P], U32) for ca in pieces}
         xr_scale = {ca: kept("xr_scale%d%d" % ca, [P, PACK, P], U8) for ca in pieces}
         g_sb = [kept("g_sb%d" % c, [P, PACK, M], F32) for c in range(CHUNKS)]
@@ -61,10 +67,15 @@ def tile_mix_xres_tm_pl_mul_kernel(
         nc.vector.memset(w_scale[:].bitcast(I32), 0)
         nc.vector.memset(x4_scale_in[:].bitcast(I32), 0)
 
-        def load_scales(plane, rows, queue, lo=0, hi=4):
-            by_row = rows.rearrange("a (q s) n -> s q a n", s=4)
-            for s in range(lo, hi):
-                queue.dma_start(out=plane[:].bitcast(I32)[s:P:32], in_=by_row[s].bitcast(I32))
+        def load_codes(dst, words):
+            nc.sync.dma_start(out=dst[:].bitcast(I32), in_=words.rearrange("a p c -> p a c").bitcast(I32))
+
+        def load_scales(plane, rows):
+            by_row = rows.rearrange("a (u s) n -> s u a n", s=GROUP_ROWS)
+            for s in range(GROUP_ROWS):
+                nc.scalar.dma_start(out=plane[:].bitcast(I32)[s:P:QUADRANT], in_=by_row[s].bitcast(I32))
+
+        xr_raw = {}
 
         def load_xr(a, lo, hi):
             dst = kept("xr_raw%d%d" % (a, lo), [P, PACK, (hi - lo) * SPAN], F32)
@@ -77,26 +88,24 @@ def tile_mix_xres_tm_pl_mul_kernel(
             rows = g[c * SPAN : (c + 1) * SPAN, :]
             nc.sync.dma_start(out=g_sb[c][:], in_=rows.rearrange("(p r) n -> p r n", r=PACK))
 
-        def load_codes(dst, words):
-            nc.sync.dma_start(out=dst[:].bitcast(I32), in_=words.rearrange("a p c -> p a c").bitcast(I32))
-
         load_codes(x4_codes_in, x4_words)
         load_codes(w_codes, w4_words)
-        load_xr(0, 0, 1)
-        load_scales(w_scale, w4_scales, nc.scalar)
-        load_scales(x4_scale_in, x4_scales, nc.scalar)
-        load_xr(1, 0, 1)
-        load_xr(2, 0, 1)
+        load_scales(w_scale, w4_scales)
+        load_scales(x4_scale_in, x4_scales)
+        for a in range(PASSES):
+            load_xr(a, 0, 1)
         load_g(0)
-        load_xr(0, 1, 3)
-        load_xr(1, 1, 3)
+        load_xr(0, 1, CHUNKS)
+        load_xr(1, 1, CHUNKS)
         load_xr(2, 1, 2)
-        load_xr(2, 2, 3)
+        load_xr(2, 2, CHUNKS)
         load_g(1)
         load_g(2)
 
+        on_vector, on_scalar = nc.vector.tensor_copy, nc.scalar.copy
+
         def deal_x4_codes(c, a):
-            nc.vector.tensor_copy(
+            on_vector(
                 out=x4_codes[c][:, a].bitcast(U16),
                 in_=x4_codes_in[:, a, 2 * SPAN * c : 2 * SPAN * (c + 1)]
                 .bitcast(U16)
@@ -104,31 +113,27 @@ def tile_mix_xres_tm_pl_mul_kernel(
             )
 
         def deal_x4_scale(c):
-            nc.vector.tensor_copy(
+            on_vector(
                 out=x4_scale[c][:],
                 in_=x4_scale_in[:, :, SPAN * c : SPAN * (c + 1)].rearrange("p a (m r) -> p r a m", r=PACK),
             )
 
         xr_bf = {}
-        on_vector, on_scalar = nc.vector.tensor_copy, nc.scalar.copy
 
-        def group_part(copy, c, a, lo, hi):
-            if (c, a) not in xr_bf:
-                xr_bf.setdefault((c, a), stage.tile([P, PACK, P, PACK], BF16, name="grouped", align_bytes=256))
-            dst = xr_bf[c, a][:].rearrange("p r m j -> p m j r")
+        def round_piece(c, a, share=PIECE_SHARE):
+            grouped = stage.tile([P, PACK, P, PACK], BF16, name="grouped", align_bytes=ALIGN)
+            dst = grouped[:].rearrange("p r m j -> p m j r")
             src = xr_raw[c, a].rearrange("p j (m r) -> p m j r", r=PACK)
-            copy(out=dst[:, lo:hi], in_=src[:, lo:hi])
+            on_vector(out=dst[:, :share], in_=src[:, :share])
+            if share < P:
+                on_scalar(out=dst[:, share:], in_=src[:, share:])
+            xr_bf.setdefault((c, a), grouped)
 
-        def group_xr(c, a, share):
-            group_part(on_vector, c, a, 0, share)
-            group_part(on_scalar, c, a, share, P)
-
-        def quantize_xr(c, a):
-            grouped = xr_bf[c, a]
+        def quantize_piece(c, a):
             nc.vector.quantize_mx(
                 out=xr_codes[c, a][:].rearrange("p r m -> p (r m)").bitcast(FP8X4),
                 scales=xr_scale[c, a][:].rearrange("p r m -> p (r m)"),
-                in_=grouped[:].rearrange("p r m j -> p (r m j)"),
+                in_=xr_bf[c, a][:].rearrange("p r m j -> p (r m j)"),
             )
 
         passes_done = {}
@@ -146,17 +151,17 @@ def tile_mix_xres_tm_pl_mul_kernel(
                 stop=len(done) == 2 * PASSES,
             )
 
-        def x4_passes(c, slots):
-            for r in slots:
+        def x4_passes(c):
+            for r in range(PACK):
                 for a in range(PASSES):
                     mx_pass(c, r, a, x4_codes[c][:, a, r, :].bitcast(FP4X4), x4_scale[c][:, r, a, :])
 
-        def xr_passes(c, a, slots):
-            for r in slots:
+        def xr_passes(c, a):
+            for r in range(PACK):
                 mx_pass(c, r, a, xr_codes[c, a][:, r, :].bitcast(FP8X4), xr_scale[c, a][:, r, :])
 
-        def gate(c, slots, lo=0, hi=M):
-            for r in slots:
+        def times_g(c, lo, hi):
+            for r in range(PACK):
                 nc.vector.tensor_tensor(
                     out=res[c][:, r, lo:hi],
                     in0=sum_bank(c, r)[:, lo:hi],
@@ -170,91 +175,81 @@ def tile_mix_xres_tm_pl_mul_kernel(
                 in_=res[c][:, :, lo:hi].rearrange("p r (u v) -> p u r v", v=4),
             )
 
-        def quantize_result(c, lo=0, hi=M):
+        def quantize_result(c, lo, hi):
             nc.vector.quantize_mx(
                 out=res_codes[:, c, lo:hi].bitcast(FP8X4),
-                scales=res_scale[SCALE_ROW:, c, lo:hi],
+                scales=res_scale[RESULT_PLANE:, c, lo:hi],
                 in_=res_bf[c][:, lo:hi, :].rearrange("p n r -> p (n r)"),
             )
-
-        def store_result(lo, hi):
-            rows = out_0[lo * SPAN : hi * SPAN, :].rearrange("(c p r) n -> p c (r n)", p=P, r=PACK)
-            nc.sync.dma_start(out=rows, in_=res_all[:, lo * PACK * M : hi * PACK * M].rearrange("p (c x) -> p c x", x=PACK * M))
-
-        def store_slots(c, lo, hi):
-            rows = out_0[c * SPAN : (c + 1) * SPAN, :].rearrange("(p r) n -> p (r n)", r=PACK)
-            first = c * PACK * M
-            nc.sync.dma_start(out=rows[:, lo * M : hi * M], in_=res_all[:, first + lo * M : first + hi * M])
-
-        def store_columns(c, lo, hi):
-            rows = out_0[c * SPAN : (c + 1) * SPAN, lo:hi].rearrange("(p r) n -> p r n", r=PACK)
-            nc.sync.dma_start(out=rows, in_=res[c][:, :, lo:hi])
-
-        def store_codes(lo, hi):
-            nc.sync.dma_start(
-                out=out_1[lo:hi].rearrange("c p n r -> p c (n r)").bitcast(I32), in_=res_codes[:, lo:hi, :].bitcast(I32)
-            )
-
-        every = range(PACK)
-
-        share = 64
 
         for c in range(CHUNKS):
             for a in range(PASSES):
                 deal_x4_codes(c, a)
-        group_part(on_vector, 0, 0, 0, P)
-        quantize_xr(0, 0)
+        round_piece(0, 0, share=P)
+        quantize_piece(0, 0)
         deal_x4_scale(0)
-        xr_passes(0, 0, every)
-        x4_passes(0, every)
+        xr_passes(0, 0)
+        x4_passes(0)
         for a in (1, 2):
-            group_xr(0, a, share)
+            round_piece(0, a)
             deal_x4_scale(a)
-            quantize_xr(0, a)
-            xr_passes(0, a, every)
-        x4_passes(1, every)
-        gate(0, every)
-        x4_passes(2, every)
-        round_result(on_scalar, 0, 256, M)
-        round_result(on_vector, 0, 0, 256)
-        group_xr(1, 0, 64)
-        quantize_result(0)
-        group_xr(2, 0, 64)
-        quantize_xr(1, 0)
-        xr_passes(1, 0, every)
-        quantize_xr(2, 0)
-        xr_passes(2, 0, every)
-        group_xr(1, 1, 64)
-        group_xr(2, 1, 64)
-        quantize_xr(1, 1)
-        xr_passes(1, 1, every)
-        group_xr(1, 2, 64)
-        quantize_xr(2, 1)
-        quantize_xr(1, 2)
-        xr_passes(1, 2, every)
-        xr_passes(2, 1, every)
-        group_xr(2, 2, 64)
-        quantize_xr(2, 2)
-        xr_passes(2, 2, every)
-        half = M // 2
-        for c in (1, 2):
-            gate(c, every, 0, half)
-            round_result(on_scalar, c, 0, half)
-            gate(c, every, half, M)
-            if c == 1:
-                round_result(on_scalar, c, half, M)
-        round_result(on_scalar, 2, 416, M)
-        quantize_result(1)
-        round_result(on_vector, 2, half, 416)
-        quantize_result(2, 0, half)
-        quantize_result(2, half, M)
+            quantize_piece(0, a)
+            xr_passes(0, a)
+        x4_passes(1)
+        times_g(0, 0, M)
+        x4_passes(2)
+        round_result(on_scalar, 0, HALF, M)
+        round_result(on_vector, 0, 0, HALF)
 
-        store_result(0, 1)
+        round_piece(1, 0)
+        quantize_result(0, 0, M)
+        round_piece(2, 0)
+        quantize_piece(1, 0)
+        xr_passes(1, 0)
+        quantize_piece(2, 0)
+        xr_passes(2, 0)
+        round_piece(1, 1)
+        round_piece(2, 1)
+        quantize_piece(1, 1)
+        xr_passes(1, 1)
+        round_piece(1, 2)
+        quantize_piece(2, 1)
+        quantize_piece(1, 2)
+        xr_passes(1, 2)
+        xr_passes(2, 1)
+        round_piece(2, 2)
+        quantize_piece(2, 2)
+        xr_passes(2, 2)
+
+        times_g(1, 0, HALF)
+        round_result(on_scalar, 1, 0, HALF)
+        times_g(1, HALF, M)
+        round_result(on_scalar, 1, HALF, M)
+        times_g(2, 0, HALF)
+        round_result(on_scalar, 2, 0, HALF)
+        times_g(2, HALF, M)
+        round_result(on_scalar, 2, LAST_SPLIT, M)
+        quantize_result(1, 0, M)
+        round_result(on_vector, 2, HALF, LAST_SPLIT)
+        quantize_result(2, 0, HALF)
+        quantize_result(2, HALF, M)
+
+        def store_result(c):
+            rows = out_0[c * SPAN : (c + 1) * SPAN, :].rearrange("(p r) n -> p r n", r=PACK)
+            nc.sync.dma_start(out=rows, in_=res[c])
+
+        def store_codes(lo, hi):
+            words = out_1[lo:hi].rearrange("c p n r -> p c (n r)")
+            nc.sync.dma_start(out=words.bitcast(I32), in_=res_codes[:, lo:hi, :].bitcast(I32))
+
+        store_result(0)
         store_codes(0, 1)
-        for c in (1, 2):
-            store_columns(c, 0, half)
-            store_columns(c, half, M)
-        store_codes(1, 3)
-        by_row = out_2.rearrange("a (q s) n -> s q a n", s=4)
-        for s in range(4):
-            nc.scalar.dma_start(out=by_row[s].bitcast(I32), in_=res_scale[:].bitcast(I32)[SCALE_ROW + s : P : 32])
+        store_result(1)
+        store_result(2)
+        store_codes(1, CHUNKS)
+
+        by_row = out_2.rearrange("c (u s) n -> s u c n", s=GROUP_ROWS)
+        for s in range(GROUP_ROWS):
+            nc.scalar.dma_start(
+                out=by_row[s].bitcast(I32), in_=res_scale[:].bitcast(I32)[RESULT_PLANE + s : P : QUADRANT]
+            )

@@ -88,17 +88,18 @@ def tile_mix_xres_tm_pl_mul_kernel(
             rows = g[c * SPAN : (c + 1) * SPAN, :]
             nc.sync.dma_start(out=g_sb[c][:], in_=rows.rearrange("(p r) n -> p r n", r=PACK))
 
-        load_codes(x4_codes_in, x4_words)
-        load_codes(w_codes, w4_words)
         load_scales(w_scale, w4_scales)
         load_scales(x4_scale_in, x4_scales)
-        for a in range(PASSES):
-            load_xr(a, 0, 1)
+        load_codes(x4_codes_in, x4_words)
+        load_xr(0, 0, 1)
+        load_codes(w_codes, w4_words)
+        load_xr(1, 0, 1)
+        load_xr(2, 0, 1)
         load_g(0)
-        load_xr(0, 1, CHUNKS)
-        load_xr(1, 1, CHUNKS)
+        load_xr(0, 1, 3)
+        load_xr(1, 1, 3)
         load_xr(2, 1, 2)
-        load_xr(2, 2, CHUNKS)
+        load_xr(2, 2, 3)
         load_g(1)
         load_g(2)
 
@@ -182,30 +183,33 @@ def tile_mix_xres_tm_pl_mul_kernel(
                 in_=res_bf[c][:, lo:hi, :].rearrange("p n r -> p (n r)"),
             )
 
-        for c in range(CHUNKS):
-            for a in range(PASSES):
+        for c in range(3):
+            for a in range(3):
                 deal_x4_codes(c, a)
-        round_piece(0, 0, share=P)
+        round_piece(0, 0, 128)
         quantize_piece(0, 0)
         deal_x4_scale(0)
         xr_passes(0, 0)
         x4_passes(0)
-        for a in (1, 2):
-            round_piece(0, a)
-            deal_x4_scale(a)
-            quantize_piece(0, a)
-            xr_passes(0, a)
+        round_piece(0, 1)
+        deal_x4_scale(1)
+        quantize_piece(0, 1)
+        xr_passes(0, 1)
+        round_piece(0, 2)
+        quantize_piece(0, 2)
+        xr_passes(0, 2)
+        deal_x4_scale(2)
         x4_passes(1)
-        times_g(0, 0, M)
-        x4_passes(2)
+        times_g(0, 0, HALF)
+        round_result(on_scalar, 0, 0, HALF)
+        times_g(0, HALF, M)
         round_result(on_scalar, 0, HALF, M)
-        round_result(on_vector, 0, 0, HALF)
-
-        round_piece(1, 0)
-        quantize_result(0, 0, M)
+        x4_passes(2)
+        round_piece(1, 0, 96)
         round_piece(2, 0)
         quantize_piece(1, 0)
         xr_passes(1, 0)
+        quantize_result(0, 0, M)
         quantize_piece(2, 0)
         xr_passes(2, 0)
         round_piece(1, 1)
@@ -220,7 +224,6 @@ def tile_mix_xres_tm_pl_mul_kernel(
         round_piece(2, 2)
         quantize_piece(2, 2)
         xr_passes(2, 2)
-
         times_g(1, 0, HALF)
         round_result(on_scalar, 1, 0, HALF)
         times_g(1, HALF, M)
@@ -246,7 +249,7 @@ def tile_mix_xres_tm_pl_mul_kernel(
         store_codes(0, 1)
         store_result(1)
         store_result(2)
-        store_codes(1, CHUNKS)
+        store_codes(1, 3)
 
         by_row = out_2.rearrange("c (u s) n -> s u c n", s=GROUP_ROWS)
         for s in range(GROUP_ROWS):

@@ -26,7 +26,7 @@ RESULT_PLANE = 4
 STAGE_BUFS = 4
 HALF = M // 2
 PIECE_SHARE = 72
-LAST_SPLIT = 416
+GAP_SPLIT = 128
 
 
 def tile_mix_xres_tm_pl_mul_kernel(
@@ -161,8 +161,16 @@ def tile_mix_xres_tm_pl_mul_kernel(
             for r in range(PACK):
                 mx_pass(c, r, a, xr_codes[c, a][:, r, :].bitcast(FP8X4), xr_scale[c, a][:, r, :])
 
-        def times_g(c, lo, hi):
-            for r in range(PACK):
+        def copy_first_slot(c):
+            nc.scalar.copy(out=res[c][:, 0, :], in_=sum_bank(c, 0)[:])
+
+        def first_slot_times_g(c):
+            nc.gpsimd.tensor_tensor(
+                out=res[c][:, 0, :], in0=res[c][:, 0, :], in1=g_sb[c][:, 0, :], op=mybir.AluOpType.mult
+            )
+
+        def times_g(c, lo, hi, first=0):
+            for r in range(first, PACK):
                 nc.vector.tensor_tensor(
                     out=res[c][:, r, lo:hi],
                     in0=sum_bank(c, r)[:, lo:hi],
@@ -222,18 +230,19 @@ def tile_mix_xres_tm_pl_mul_kernel(
         xr_passes(1, 2)
         xr_passes(2, 1)
         round_piece(2, 2)
+        copy_first_slot(1)
         quantize_piece(2, 2)
         xr_passes(2, 2)
-        times_g(1, 0, HALF)
-        round_result(on_scalar, 1, 0, HALF)
-        times_g(1, HALF, M)
-        round_result(on_scalar, 1, HALF, M)
-        times_g(2, 0, HALF)
+        copy_first_slot(2)
+        first_slot_times_g(1)
+        times_g(1, 0, M, 1)
+        round_result(on_scalar, 1, GAP_SPLIT, M)
+        round_result(on_vector, 1, 0, GAP_SPLIT)
+        first_slot_times_g(2)
+        times_g(2, 0, M, 1)
         round_result(on_scalar, 2, 0, HALF)
-        times_g(2, HALF, M)
-        round_result(on_scalar, 2, LAST_SPLIT, M)
         quantize_result(1, 0, M)
-        round_result(on_vector, 2, HALF, LAST_SPLIT)
+        round_result(on_vector, 2, HALF, M)
         quantize_result(2, 0, HALF)
         quantize_result(2, HALF, M)
 

@@ -24,8 +24,10 @@ GROUP_ROWS = 4
 ALIGN = 256
 RESULT_PLANE = 4
 STAGE_BUFS = 4
+RUN = 4
 HALF = M // 2
 PIECE_SHARE = 72
+BUSY_SHARE = 96
 GAP_SPLIT = 128
 
 
@@ -113,10 +115,10 @@ def tile_mix_xres_tm_pl_mul_kernel(
                 .rearrange("p (m r) -> p r m", r=PACK),
             )
 
-        def deal_x4_scale(c):
+        def deal_x4_scale(c, lo=0, hi=PACK):
             on_vector(
-                out=x4_scale[c][:],
-                in_=x4_scale_in[:, :, SPAN * c : SPAN * (c + 1)].rearrange("p a (m r) -> p r a m", r=PACK),
+                out=x4_scale[c][:, lo:hi],
+                in_=x4_scale_in[:, :, SPAN * c : SPAN * (c + 1)].rearrange("p a (m r) -> p r a m", r=PACK)[:, lo:hi],
             )
 
         xr_bf = {}
@@ -180,8 +182,8 @@ def tile_mix_xres_tm_pl_mul_kernel(
 
         def round_result(copy, c, lo, hi):
             copy(
-                out=res_bf[c][:, lo:hi, :].rearrange("p (u v) r -> p u r v", v=4),
-                in_=res[c][:, :, lo:hi].rearrange("p r (u v) -> p u r v", v=4),
+                out=res_bf[c][:, lo:hi, :].rearrange("p (n v) r -> p n r v", v=RUN),
+                in_=res[c][:, :, lo:hi].rearrange("p r (n v) -> p n r v", v=RUN),
             )
 
         def quantize_result(c, lo, hi):
@@ -191,12 +193,13 @@ def tile_mix_xres_tm_pl_mul_kernel(
                 in_=res_bf[c][:, lo:hi, :].rearrange("p n r -> p (n r)"),
             )
 
-        for c in range(3):
-            for a in range(3):
+        for c in range(CHUNKS):
+            for a in range(PASSES):
                 deal_x4_codes(c, a)
-        round_piece(0, 0, 128)
+        round_piece(0, 0, P)
         quantize_piece(0, 0)
-        deal_x4_scale(0)
+        deal_x4_scale(0, 0, PACK // 2)
+        deal_x4_scale(0, PACK // 2, PACK)
         xr_passes(0, 0)
         x4_passes(0)
         round_piece(0, 1)
@@ -207,13 +210,15 @@ def tile_mix_xres_tm_pl_mul_kernel(
         quantize_piece(0, 2)
         xr_passes(0, 2)
         deal_x4_scale(2)
+
         x4_passes(1)
         times_g(0, 0, HALF)
         round_result(on_scalar, 0, 0, HALF)
         times_g(0, HALF, M)
         round_result(on_scalar, 0, HALF, M)
         x4_passes(2)
-        round_piece(1, 0, 96)
+
+        round_piece(1, 0, BUSY_SHARE)
         round_piece(2, 0)
         quantize_piece(1, 0)
         xr_passes(1, 0)
@@ -234,12 +239,14 @@ def tile_mix_xres_tm_pl_mul_kernel(
         quantize_piece(2, 2)
         xr_passes(2, 2)
         copy_first_slot(2)
+
         first_slot_times_g(1)
         times_g(1, 0, M, 1)
         round_result(on_scalar, 1, GAP_SPLIT, M)
         round_result(on_vector, 1, 0, GAP_SPLIT)
         first_slot_times_g(2)
         times_g(2, 0, M, 1)
+
         round_result(on_scalar, 2, 0, HALF)
         quantize_result(1, 0, M)
         round_result(on_vector, 2, HALF, M)

from contextlib import ExitStack

import concourse.mybir as mybir

K, M, T = 1536, 512, 1536
FLOPS = 2 * 2 * K * M * T

F32 = mybir.dt.float32
BF16 = mybir.dt.bfloat16
I32 = mybir.dt.int32
U32 = mybir.dt.uint32
U8 = mybir.dt.uint8
U16 = mybir.dt.uint16
FP8X4 = mybir.dt.float8_e4m3fn_x4
FP4X4 = mybir.dt.float4_e2m1fn_x4

P = 128
PACK = 4
SPAN = P * PACK
PASSES = K // SPAN
CHUNKS = T // SPAN
QUADRANT = 32
GROUP_ROWS = 4
ALIGN = 256
RESULT_PLANE = 4
STAGE_BUFS = 4
RUN = 4
HALF = M // 2
PIECE_SHARE = 72
BUSY_SHARE = 96
GAP_SPLIT = 128


def tile_mix_xres_tm_pl_mul_kernel(
    tc, x4_words, x4_scales, xr, w4_words, w4_scales, g, out_0, out_1, out_2
):
    nc = tc.nc
    with ExitStack() as ctx:
        keep = ctx.enter_context(tc.tile_pool(name="keep", bufs=1))
        stage = ctx.enter_context(tc.tile_pool(name="stage", bufs=STAGE_BUFS))
        psum = ctx.enter_context(tc.psum_pool(name="psum", bufs=1))
        ctx.enter_context(tc.manual_schedule())

        def kept(name, shape, dtype):
            return keep.tile(shape, dtype, name=name, align_bytes=ALIGN)

        w_codes = kept("w_codes", [P, PASSES, 2 * M], U8)
        w_scale = kept("w_scale", [P, PASSES, M], U8)
        x4_codes_in = kept("x4_codes_in", [P, PASSES, 2 * T], U8)
        x4_scale_in = kept("x4_scale_in", [P, PASSES, T], U8)
        x4_codes = [kept("x4_codes%d" % c, [P, PASSES, PACK, 2 * P], U8) for c in range(CHUNKS)]
        x4_scale = [kept("x4_scale%d" % c, [P, PACK, PASSES, P], U8) for c in range(CHUNKS)]
        pieces = [(c, a) for c in range(CHUNKS) for a in range(PASSES)]
        xr_codes = {ca: kept("xr_codes%d%d" % ca, [P, PACK, P], U32) for ca in pieces}
        xr_scale = {ca: kept("xr_scale%d%d" % ca, [P, PACK, P], U8) for ca in pieces}
        g_sb = [kept("g_sb%d" % c, [P, PACK, M], F32) for c in range(CHUNKS)]
        res_all = kept("res_all", [P, CHUNKS * PACK * M], F32)
        res = [
            res_all[:, c * PACK * M : (c + 1) * PACK * M].rearrange("p (r n) -> p r n", r=PACK) for c in range(CHUNKS)
        ]
        res_bf = [kept("res_bf%d" % c, [P, M, PACK], BF16) for c in range(CHUNKS)]
        res_codes = kept("res_codes", [P, CHUNKS, M], U32)
        res_scale = kept("res_scale", [P, CHUNKS, M], U8)
        banks = [psum.tile([P, M], F32, name="bank%d" % i) for i in range(2 * PACK)]

        def sum_bank(c, r):
            return banks[PACK * (c % 2) + r]

        nc.vector.memset(w_scale[:].bitcast(I32), 0)
        nc.vector.memset(x4_scale_in[:].bitcast(I32), 0)

        def load_codes(dst, words):
            nc.sync.dma_start(out=dst[:].bitcast(I32), in_=words.rearrange("a p c -> p a c").bitcast(I32))

        def load_scales(plane, rows):
            by_row = rows.rearrange("a (u s) n -> s u a n", s=GROUP_ROWS)
            for s in range(GROUP_ROWS):
                nc.scalar.dma_start(out=plane[:].bitcast(I32)[s:P:QUADRANT], in_=by_row[s].bitcast(I32))

        xr_raw = {}

        def load_xr(a, lo, hi):
            dst = kept("xr_raw%d%d" % (a, lo), [P, PACK, (hi - lo) * SPAN], F32)
            rows = xr[a * SPAN : (a + 1) * SPAN, lo * SPAN : hi * SPAN]
            nc.sync.dma_start(out=dst[:], in_=rows.rearrange("(p j) t -> p j t", j=PACK))
            for c in range(lo, hi):
                xr_raw.setdefault((c, a), dst[:, :, (c - lo) * SPAN : (c - lo + 1) * SPAN])

        def load_g(c):
            rows = g[c * SPAN : (c + 1) * SPAN, :]
            nc.sync.dma_start(out=g_sb[c][:], in_=rows.rearrange("(p r) n -> p r n", r=PACK))

        load_scales(w_scale, w4_scales)
        load_scales(x4_scale_in, x4_scales)
        load_codes(x4_codes_in, x4_words)
        load_xr(0, 0, 1)
        load_codes(w_codes, w4_words)
        load_xr(1, 0, 1)
        load_xr(2, 0, 1)
        load_g(0)
        load_xr(0, 1, 3)
        load_xr(1, 1, 3)
        load_xr(2, 1, 2)
        load_xr(2, 2, 3)
        load_g(1)
        load_g(2)

        on_vector, on_scalar = nc.vector.tensor_copy, nc.scalar.copy

        def deal_x4_codes(c, a):
            on_vector(
                out=x4_codes[c][:, a].bitcast(U16),
                in_=x4_codes_in[:, a, 2 * SPAN * c : 2 * SPAN * (c + 1)]
                .bitcast(U16)
                .rearrange("p (m r) -> p r m", r=PACK),
            )

        def deal_x4_scale(c, lo=0, hi=PACK):
            on_vector(
                out=x4_scale[c][:, lo:hi],
                in_=x4_scale_in[:, :, SPAN * c : SPAN * (c + 1)].rearrange("p a (m r) -> p r a m", r=PACK)[:, lo:hi],
            )

        xr_bf = {}

        def round_piece(c, a, share=PIECE_SHARE):
            grouped = stage.tile([P, PACK, P, PACK], BF16, name="grouped", align_bytes=ALIGN)
            dst = grouped[:].rearrange("p r m j -> p m j r")
            src = xr_raw[c, a].rearrange("p j (m r) -> p m j r", r=PACK)
            on_vector(out=dst[:, :share], in_=src[:, :share])
            if share < P:
                on_scalar(out=dst[:, share:], in_=src[:, share:])
            xr_bf.setdefault((c, a), grouped)

        def quantize_piece(c, a):
            nc.vector.quantize_mx(
                out=xr_codes[c, a][:].rearrange("p r m -> p (r m)").bitcast(FP8X4),
                scales=xr_scale[c, a][:].rearrange("p r m -> p (r m)"),
                in_=xr_bf[c, a][:].rearrange("p r m j -> p (r m j)"),
            )

        passes_done = {}

        def mx_pass(c, r, a, lhsT, lhsT_scale):
            done = passes_done.setdefault((c, r), [])
            done.append(a)
            nc.tensor.matmul_mx(
                out=sum_bank(c, r)[:],
                lhsT=lhsT,
                lhsT_scale=lhsT_scale,
                rhs=w_codes[:, a, :].bitcast(FP4X4),
                rhs_scale=w_scale[:, a, :],
                start=len(done) == 1,
                stop=len(done) == 2 * PASSES,
            )

        def x4_passes(c):
            for r in range(PACK):
                for a in range(PASSES):
                    mx_pass(c, r, a, x4_codes[c][:, a, r, :].bitcast(FP4X4), x4_scale[c][:, r, a, :])

        def xr_passes(c, a):
            for r in range(PACK):
                mx_pass(c, r, a, xr_codes[c, a][:, r, :].bitcast(FP8X4), xr_scale[c, a][:, r, :])

        def copy_first_slot(c):
            nc.scalar.copy(out=res[c][:, 0, :], in_=sum_bank(c, 0)[:])

        def first_slot_times_g(c):
            nc.gpsimd.tensor_tensor(
                out=res[c][:, 0, :], in0=res[c][:, 0, :], in1=g_sb[c][:, 0, :], op=mybir.AluOpType.mult
            )

        def times_g(c, lo, hi, first=0):
            for r in range(first, PACK):
                nc.vector.tensor_tensor(
                    out=res[c][:, r, lo:hi],
                    in0=sum_bank(c, r)[:, lo:hi],
                    in1=g_sb[c][:, r, lo:hi],
                    op=mybir.AluOpType.mult,
                )

        def round_result(copy, c, lo, hi):
            copy(
                out=res_bf[c][:, lo:hi, :].rearrange("p (n v) r -> p n r v", v=RUN),
                in_=res[c][:, :, lo:hi].rearrange("p r (n v) -> p n r v", v=RUN),
            )

        def quantize_result(c, lo, hi):
            nc.vector.quantize_mx(
                out=res_codes[:, c, lo:hi].bitcast(FP8X4),
                scales=res_scale[RESULT_PLANE:, c, lo:hi],
                in_=res_bf[c][:, lo:hi, :].rearrange("p n r -> p (n r)"),
            )

        for c in range(CHUNKS):
            for a in range(PASSES):
                deal_x4_codes(c, a)
        round_piece(0, 0, P)
        quantize_piece(0, 0)
        deal_x4_scale(0, 0, PACK // 2)
        deal_x4_scale(0, PACK // 2, PACK)
        xr_passes(0, 0)
        x4_passes(0)
        round_piece(0, 1)
        deal_x4_scale(1)
        quantize_piece(0, 1)
        xr_passes(0, 1)
        round_piece(0, 2)
        quantize_piece(0, 2)
        xr_passes(0, 2)
        deal_x4_scale(2)

        x4_passes(1)
        times_g(0, 0, HALF)
        round_result(on_scalar, 0, 0, HALF)
        times_g(0, HALF, M)
        round_result(on_scalar, 0, HALF, M)
        x4_passes(2)

        round_piece(1, 0, BUSY_SHARE)
        round_piece(2, 0)
        quantize_piece(1, 0)
        xr_passes(1, 0)
        quantize_result(0, 0, M)
        quantize_piece(2, 0)
        xr_passes(2, 0)
        round_piece(1, 1)
        round_piece(2, 1)
        quantize_piece(1, 1)
        xr_passes(1, 1)
        round_piece(1, 2)
        quantize_piece(2, 1)
        quantize_piece(1, 2)
        xr_passes(1, 2)
        xr_passes(2, 1)
        round_piece(2, 2)
        copy_first_slot(1)
        quantize_piece(2, 2)
        xr_passes(2, 2)
        copy_first_slot(2)

        first_slot_times_g(1)
        times_g(1, 0, M, 1)
        round_result(on_scalar, 1, GAP_SPLIT, M)
        round_result(on_vector, 1, 0, GAP_SPLIT)
        first_slot_times_g(2)
        times_g(2, 0, M, 1)

        round_result(on_scalar, 2, 0, HALF)
        quantize_result(1, 0, M)
        round_result(on_vector, 2, HALF, M)
        quantize_result(2, 0, HALF)
        quantize_result(2, HALF, M)

        def store_result(c):
            rows = out_0[c * SPAN : (c + 1) * SPAN, :].rearrange("(p r) n -> p r n", r=PACK)
            nc.sync.dma_start(out=rows, in_=res[c])

        def store_codes(lo, hi):
            words = out_1[lo:hi].rearrange("c p n r -> p c (n r)")
            nc.sync.dma_start(out=words.bitcast(I32), in_=res_codes[:, lo:hi, :].bitcast(I32))

        store_result(0)
        store_codes(0, 1)
        store_result(1)
        store_result(2)
        store_codes(1, 3)

        by_row = out_2.rearrange("c (u s) n -> s u c n", s=GROUP_ROWS)
        for s in range(GROUP_ROWS):
            nc.scalar.dma_start(
                out=by_row[s].bitcast(I32), in_=res_scale[:].bitcast(I32)[RESULT_PLANE + s : P : QUADRANT]
            )
